import numpy as np, ml_dtypes
CORES = [2,3,42,43,82,83,122,123]
N = 8
import mx_ref
BF = ml_dtypes.bfloat16
def entries(a):
    return np.ascontiguousarray(a.T).reshape(-1)
def table(e):
    return np.ascontiguousarray(np.reshape(e, (-1, 16)).T).astype(np.int32)
def cols(t, e):
    v = np.concatenate([t.reshape(128, -1, 4), np.zeros((128, 1, 4), BF)], axis=1)
    return np.ascontiguousarray(v[:, e]).reshape(128, -1)
def f(rng, *shape):
    return mx_ref.flush((rng.standard_normal(shape, dtype=np.float32) * np.exp2(rng.integers(-2, 3, shape[:-1] + (1,)))).astype(BF))
def wide(rng, *shape, cols=0):
    v = rng.standard_normal(shape, dtype=np.float32) * np.exp2(rng.integers(-12, 13, shape)).astype(np.float32)
    if cols: v *= np.repeat(np.exp2(rng.integers(-cols, cols + 1, shape[:-2] + (1, shape[-1] // 4))) * (rng.random(shape[:-2] + (1, shape[-1] // 4)) > 0.0625), 4, axis=-1).astype(np.float32)
    return mx_ref.flush(v.astype(BF))
T, KP, TOT, QT = 512, 320, 2048, 8
CAPP, DR, CW = KP // N, T // 16, TOT // N
def counts(rng, lo, hi):
    L, U = [TOT], [TOT]
    for q in range(N)[::-1]:
        L.insert(0, max(q * CW - N * DR, L[0] - hi[q]))
        U.insert(0, min((q - 1) * CW + N * (DR + CAPP + 1), U[0] - lo[q]))
    n, s = [], 0
    for q in range(N):
        n.append(int(rng.integers(max(lo[q], L[q + 1] - s), min(hi[q], U[q + 1] - s) + 1))); s += n[-1]
    return n
def slots(k):
    s, p, g = np.full((N, N, CAPP), -1), np.zeros((N, CW), int), 0
    for q in range(N):
        used = [0] * N
        for c in k[q]:
            r = g % N
            s[q, r, used[r]] = c; p[r, g // N] = q * CAPP + used[r]
            used[r] += 1; g += 1
    return np.stack([table(a) for a in s]), np.stack([table(a) for a in p])
def lists(rng, lo=None, hi=None, front=False):
    n = counts(rng, [3 * T // 8] * N if lo is None else lo, [KP] * N if hi is None else hi)
    k = [np.arange(m) if front else np.sort(rng.choice(T, m, replace=False)) for m in n]
    s, p = slots(k)
    return {"kept": np.stack([table(np.concatenate([a, np.full(KP - len(a), -1)])) for a in k]), "snd": s, "pl": p}
def setup_inputs(rng):
    return {"x": f(rng, N, 128, 4 * T), "qw": f(rng, N, 128, QT * 512), **lists(rng)}
def setup_inputs_few(rng):
    return {**setup_inputs(rng), **lists(rng, [T // 2] * (N - 1) + [1], [KP] * (N - 1) + [N])}
def setup_inputs_front(rng):
    return {**setup_inputs(rng), **lists(rng, front=True)}
def setup_inputs_none(rng):
    return {**setup_inputs(rng), **lists(rng, [0] + [T // 2] * (N - 1), [0] + [KP] * (N - 1))}
def setup_inputs_spread(rng):
    d = setup_inputs(rng); d["x"] = wide(rng, N, 128, 4 * T); return d
def setup_inputs_steep(rng):
    d = {**setup_inputs(rng), **lists(rng, [KP] * 5 + [CW + 1, 1, 1], [KP] * 5 + [CW + N, KP, KP])}
    assert (int((d["kept"][:6] >= 0).sum()) - 1) // N - 5 * (CW // N) == DR + CAPP
    return d
def check_inputs(d):
    b, k = [], []
    for q in range(N):
        e = entries(d["kept"][q]); n = int((e >= 0).sum()); k.append(e[:n])
        if e.min() < -1 or e.max() >= T or (e[:n] < 0).any() or (e[n:] != -1).any() or (np.diff(e[:n]) <= 0).any(): b.append("kept")
    if sum(len(a) for a in k) != TOT: b.append("sum of n_q")
    if b: return b
    g = 0
    for q in range(N):
        a = np.arange(g, g + len(k[q])); g += len(k[q])
        if len(a) == 0: continue
        if np.bincount(a % N).max() > CAPP: b.append("columns of a pair")
        p = a // N - q * TOT // (N * N)
        if p.min() < -DR or p.max() > DR + CAPP: b.append("drift")
    s, p = slots(k)
    if not np.array_equal(s, d["snd"]): b.append("snd")
    if not np.array_equal(p, d["pl"]): b.append("pl")
    return b
def reference(x, qw, kept, snd, pl):
    v = []
    for q in range(N):
        e = entries(kept[q]); v.append(cols(x[q], e[e >= 0]))
    v = np.concatenate(v, axis=1)
    y = np.zeros((N, 128, QT * CW), np.float32)
    for r in range(N):
        C = mx_ref.quantize(cols(v, np.arange(r, TOT, N)))
        for o in range(QT): y[r][:, CW * o:CW * o + CW] = mx_ref.matmul(mx_ref.quantize(qw[r][:, 512 * o:512 * o + 512]), C)
    return {"y": y}

@@ -1,0 +1,228 @@
+from concourse.bass import DstId, RemoteDMATransfer
+from concourse.mybir import dt, AluOpType, ActivationFunctionType
+
+N, TC, KP, CAPP, DR, CW, QT = 8, 512, 320, 40, 32, 256, 8
+HALF = N // 2
+HS = HALF * CAPP
+EARLY = KP - 2 * CAPP
+LM = 128
+
+SCRATCH = {
+    "xs": ("sbuf", [128, 4 * TC], "bfloat16"),
+    "sl": ("sbuf", [128, KP // 16], "int32"),
+    "of0": ("sbuf", [128, KP // 16], "uint16"),
+    "of1": ("sbuf", [128, KP // 16], "uint16"),
+    "of2": ("sbuf", [128, KP // 16], "uint16"),
+    "of3": ("sbuf", [128, KP // 16], "uint16"),
+    "tf": ("sbuf", [128, 4 * HS], "bfloat16"),
+    "tn": ("sbuf", [128, 4 * HS], "bfloat16"),
+    "qfc": ("sbuf", [128, HS], "float8_e4m3fn_x4"),
+    "qfs": ("sbuf", [128, HS], "uint8"),
+    "qnc": ("sbuf", [128, HS], "float8_e4m3fn_x4"),
+    "qns": ("sbuf", [128, HS], "uint8"),
+    "lc": ("sbuf", [128, KP], "float8_e4m3fn_x4"),
+    "ls": ("sbuf", [128, KP], "uint8"),
+    "pls": ("sbuf", [128, CW // 16], "int32"),
+    "plw": ("sbuf", [128, CW // 16], "int32"),
+    "plr": ("sbuf", [128, CW // 16], "int32"),
+    "offe": ("sbuf", [128, CW // 16], "uint16"),
+    "offl": ("sbuf", [128, CW // 16], "uint16"),
+    "qwb": ("sbuf", [128, QT * 512], "bfloat16"),
+    "qwc": ("sbuf", [128, QT * 128], "float8_e4m3fn_x4"),
+    "qws": ("sbuf", [128, QT * 128], "uint8"),
+    "ps": ("psum", [128, 512 * QT], "float32"),
+    "rs": ("sbuf", [128, KP * QT], "float32"),
+    "ysb": ("sbuf", [128, CW * QT], "float32"),
+}
+SEMAPHORES = (["xl", "sndl", "pll", "qwa", "qwb_", "own", "early", "late", "sent", "go", "store", "pa", "pb", "pc", "qf", "qn"]
+              + ["o%d" % t for t in range(4)] + ["gf%d" % t for t in range(4)] + ["gn%d" % t for t in range(4)]
+              + ["%s%d" % (a, o) for a in ("qq", "me", "ce", "ge", "ml", "cl", "gl") for o in range(QT)])
+
+COPY = ActivationFunctionType.Copy
+
+
+def late_ranks(d, T, topo):
+    h = d // HALF * HALF
+    return [q for q in range(h, h + HALF) if topo.chip(T.cores[q]) != topo.chip(T.cores[d])]
+
+
+def first(d, T, topo):
+    return (max(late_ranks(d, T, topo)) + 1) % N
+
+
+def land(d, q, T, topo):
+    return CAPP * ((q - first(d, T, topo)) % N)
+
+
+def rank_program(g, core, T, topo):
+    r = T.rank_of(core)
+    if r is None:
+        return
+    S = T.sem
+    V, A, P, Y = g.vector, g.scalar, g.tensor, g.sync
+    my = r // HALF
+    fh = 1 - my
+    far = list(range(HALF * fh, HALF * fh + HALF))
+    late = late_ranks(r, T, topo)
+    mate = [q for q in range(N) if q != r and topo.chip(T.cores[q]) == topo.chip(core)]
+    OF = [T.of0, T.of1, T.of2, T.of3]
+
+    p0 = max(0, CW // N * min(late) - DR) // 16 * 16
+    p1 = (min(CW, CW // N * max(late) + DR + CAPP + 1) + 15) // 16 * 16
+    if p1 <= CW - p0:
+        l0, l1, e0, e1 = 0, p1, p1, CW
+    else:
+        l0, l1, e0, e1 = p0, CW, 0, p0
+    le, ll = (e1 - e0) // 16, (l1 - l0) // 16
+
+    for k in range(4):
+        Y.dma_start(T.sl[16 * k:16 * k + 16, :], T.snd[:, :]).then_inc(S.sndl, 16)
+        A.dma_start(T.sl[16 * k + 64:16 * k + 80, :], T.snd[:, :]).then_inc(S.sndl, 16)
+    Y.dma_start(T.xs[:, :], T.x[:, :]).then_inc(S.xl, 16)
+    Y.dma_start(T.qwb[:, 0:2048], T.qw[:, 0:2048]).then_inc(S.qwa, 16)
+    for k in range(8):
+        Y.dma_start(T.pls[16 * k:16 * k + 16, :], T.pl[:, :]).then_inc(S.pll, 16)
+
+    V.wait_ge(S.sndl, 128)
+    for t in (2, 0, 3, 1):
+        V.tensor_scalar(OF[t][:, :], T.sl[:, :], 4.0, float(t), AluOpType.mult, AluOpType.add).then_inc(S["o%d" % t], 1)
+
+    def gather(tile, h, name, wait):
+        c = HS // 16 * h
+        for eng, t in ((V, 0), (A, 2), (V, 1), (A, 3)):
+            if wait:
+                eng.wait_ge(S["o%d" % t], 1)
+                if t % 2 == 0:
+                    eng.wait_ge(S.xl, 16)
+            src = T.xs[:, 0:4 * TC].indirect(OF[t][:, c:c + HS // 16])
+            if eng is V:
+                V.tensor_copy(tile[:, t:4 * HS:4], src).then_inc(S["%s%d" % (name, t)], 1)
+            else:
+                A.activation(tile[:, t:4 * HS:4], src, COPY).then_inc(S["%s%d" % (name, t)], 1)
+
+    gather(T.tf, fh, "gf", True)
+    for t in range(4):
+        V.wait_ge(S["gf%d" % t], 1)
+    V.quantize_mx(T.qfc[:, :], T.qfs[:, :], T.tf[:, :]).then_inc(S.qf, 1)
+    gather(T.tn, my, "gn", False)
+    for t in range(4):
+        V.wait_ge(S["gn%d" % t], 1)
+    V.quantize_mx(T.qnc[:, :], T.qns[:, :], T.tn[:, :]).then_inc(S.qn, 1)
+
+    def transfer(dst, engs, sem, codes, planes, scale):
+        rid, pid = topo.addr(T.cores[dst])[:2]
+        a, b = CAPP * (dst % HALF), land(dst, r, T, topo)
+        if scale:
+            s, d = planes[:, a:a + CAPP], T.ls[:, b:b + CAPP]
+        else:
+            s, d = codes[:, a:a + CAPP].bitcast(dt.uint8), T.lc[:, b:b + CAPP].bitcast(dt.uint8)
+        m = 0
+        for e in engs:
+            m |= 1 << e
+        return RemoteDMATransfer(dst_ids=[DstId(rid=rid, pnc=pid)], dma_engine_mask=m, remote_sem=sem, src=s, dst=d)
+
+    g.wait_ge(S.qf, 1)
+    sent = 0
+    for scale in (False, True):
+        tr = []
+        for i, d in enumerate(far):
+            e = topo.engines(core, T.cores[d])
+            w = len(e) // len(far)
+            tr.append(transfer(d, e[w * i:w * i + w], S.early, T.qfc, T.qfs, scale))
+            sent += w
+        g.remote_dma_fused(tr, local_sem=S.sent)
+    g.wait_ge(S.qn, 1)
+    for scale in (False, True):
+        tr, used = [], []
+        for i, d in enumerate(late):
+            e = topo.engines(core, T.cores[d])
+            w = len(e) // len(late)
+            tr.append(transfer(d, e[w * i:w * i + w], S.late, T.qnc, T.qns, scale))
+            used += e[w * i:w * i + w]
+        for d in mate:
+            e = [k for k in topo.engines(core, T.cores[d]) if k not in used]
+            tr.append(transfer(d, e, S.early, T.qnc, T.qns, scale))
+            used += e
+        sent += len(used)
+        g.remote_dma_fused(tr, local_sem=S.sent)
+    g.sem_inc(S.go, 1)
+    n_early = 2 * (8 + 8)
+    n_late = 2 * 8
+
+    a, b = CAPP * (r % HALF), land(r, r, T, topo)
+    Y.wait_ge(S.qn, 1)
+    Y.dma_start(T.lc[:, b:b + CAPP].bitcast(dt.uint8), T.qnc[:, a:a + CAPP].bitcast(dt.uint8)).then_inc(S.own, 16)
+    Y.dma_start(T.ls[:, b:b + CAPP], T.qns[:, a:a + CAPP]).then_inc(S.own, 16)
+    Y.wait_ge(S.go, 1)
+    Y.dma_start(T.qwb[:, 2048:4096], T.qw[:, 2048:4096]).then_inc(S.qwb_, 16)
+
+    def quant_w(o):
+        V.quantize_mx(T.qwc[:, 128 * o:128 * o + 128], T.qws[:, 128 * o:128 * o + 128],
+                      T.qwb[:, 512 * o:512 * o + 512]).then_inc(S["qq%d" % o], 1)
+
+    V.wait_ge(S.qwa, 16)
+    V.wait_ge(S.pll, 128)
+    rot = float(CAPP * first(r, T, topo))
+    V.tensor_scalar(T.plw[:, :], T.pls[:, :], rot, float(KP), AluOpType.is_lt, AluOpType.mult).then_inc(S.pa, 1)
+    quant_w(0)
+    quant_w(1)
+    V.wait_ge(S.pa, 1)
+    V.tensor_tensor(T.plr[:, :], T.pls[:, :], T.plw[:, :], AluOpType.add).then_inc(S.pb, 1)
+    quant_w(2)
+    quant_w(3)
+    V.wait_ge(S.pb, 1)
+    V.tensor_scalar(T.offe[:, 0:le], T.plr[:, e0 // 16:e1 // 16], rot, None, AluOpType.subtract).then_inc(S.pc, 1)
+    V.tensor_scalar(T.offl[:, 0:ll], T.plr[:, l0 // 16:l1 // 16], rot, None, AluOpType.subtract).then_inc(S.pc, 1)
+    V.wait_ge(S.qwb_, 16)
+    for o in range(4, QT):
+        quant_w(o)
+
+    P.wait_ge(S.own, 32)
+    P.wait_ge(S.early, n_early)
+    for o in range(QT):
+        P.wait_ge(S["qq%d" % o], 1)
+        P.matmul_mx(T.ps[:, 512 * o:512 * o + EARLY], T.qwc[:, 128 * o:128 * o + 128], T.qws[:, 128 * o:128 * o + 128],
+                    T.lc[:, 0:EARLY], T.ls[:, 0:EARLY], True, True).then_inc(S["me%d" % o], 1)
+    P.wait_ge(S.late, n_late)
+    for o in range(QT):
+        P.wait_ge(S["ce%d" % o], 1)
+        P.matmul_mx(T.ps[:, 512 * o:512 * o + LM], T.qwc[:, 128 * o:128 * o + 128], T.qws[:, 128 * o:128 * o + 128],
+                    T.lc[:, KP - LM:KP], T.ls[:, KP - LM:KP], True, True).then_inc(S["ml%d" % o], 1)
+
+    def move(eng, out, src, sem):
+        if eng is V:
+            V.tensor_copy(out, src).then_inc(sem, 1)
+        else:
+            A.activation(out, src, COPY).then_inc(sem, 1)
+
+    def copy_early(eng, o):
+        eng.wait_ge(S["me%d" % o], 1)
+        move(eng, T.rs[:, KP * o:KP * o + EARLY], T.ps[:, 512 * o:512 * o + EARLY], S["ce%d" % o])
+
+    def gather_early(eng, o):
+        eng.wait_ge(S["ce%d" % o], 1)
+        move(eng, T.ysb[:, CW * o + e0:CW * o + e1], T.rs[:, KP * o:KP * o + EARLY].indirect(T.offe[:, 0:le]), S["ge%d" % o])
+
+    def copy_late(eng, o):
+        eng.wait_ge(S["ml%d" % o], 1)
+        move(eng, T.rs[:, KP * o + EARLY:KP * o + KP], T.ps[:, 512 * o + LM - 2 * CAPP:512 * o + LM], S["cl%d" % o])
+
+    def gather_late(eng, o):
+        eng.wait_ge(S["cl%d" % o], 1)
+        move(eng, T.ysb[:, CW * o + l0:CW * o + l1], T.rs[:, KP * o:KP * o + KP].indirect(T.offl[:, 0:ll]), S["gl%d" % o])
+
+    for eng, k in ((V, 0), (A, 1)):
+        eng.wait_ge(S.pc, 2)
+        for cp, ga in ((copy_early, gather_early), (copy_late, gather_late)):
+            cp(eng, k)
+            for o in range(k, QT - 2, 2):
+                cp(eng, o + 2)
+                ga(eng, o)
+            ga(eng, QT - 2 + k)
+
+    for name, a, b in (("ge", e0, e1), ("gl", l0, l1)):
+        for o in range(QT):
+            Y.wait_ge(S["%s%d" % (name, o)], 1)
+            Y.dma_start(T.y[:, CW * o + a:CW * o + b], T.ysb[:, CW * o + a:CW * o + b]).then_inc(S.store, 16)
+    Y.wait_ge(S.store, 16 * 2 * QT)
+    g.wait_ge(S.sent, sent)

@@ -4,12 +4,23 @@ from concourse.mybir import dt, AluOpType, ActivationFunctionType
 N, TC, KP, CAPP, DR, CW, QT = 8, 512, 320, 40, 32, 256, 8
 HALF = N // 2
 HS = HALF * CAPP
-EARLY = KP - 2 * CAPP
-LM = 128
+PS = 2 * CAPP
+LW = 448
+
+CFG = dict(
+    first="far",
+    loads=[(0, 4, "snd"), (4, 8, "snd")],
+    second_v=(0, 1),
+    v="pl:0,1,2,3,4,5,6,7 ce0 ce2 ge0 ce4 ge2 ce6 ge4 ge6 cl0 cl2 gl0 cl4 gl2 cl6 gl4 gl6",
+    a="ce1 ce3 ge1 ce5 ge3 ce7 ge5 ge7 cl1 cl3 gl1 cl5 gl3 cl7 gl5 gl7",
+    p="me0 me1 me2 me3 me4 me5 me6 me7 ml0 ml1 ml2 ml3 ml4 ml5 ml6 ml7",
+    y="O0 O2 O4 O6 P0 P2 P4 P6",
+)
 
 SCRATCH = {
     "xs": ("sbuf", [128, 4 * TC], "bfloat16"),
     "sl": ("sbuf", [128, KP // 16], "int32"),
+    "sp": ("sbuf", [128, KP // 16], "int32"),
     "of0": ("sbuf", [128, KP // 16], "uint16"),
     "of1": ("sbuf", [128, KP // 16], "uint16"),
     "of2": ("sbuf", [128, KP // 16], "uint16"),
@@ -18,15 +29,14 @@ SCRATCH = {
     "tn": ("sbuf", [128, 4 * HS], "bfloat16"),
     "qfc": ("sbuf", [128, HS], "float8_e4m3fn_x4"),
     "qfs": ("sbuf", [128, HS], "uint8"),
-    "qnc": ("sbuf", [128, HS], "float8_e4m3fn_x4"),
-    "qns": ("sbuf", [128, HS], "uint8"),
-    "lc": ("sbuf", [128, KP], "float8_e4m3fn_x4"),
-    "ls": ("sbuf", [128, KP], "uint8"),
+    "lc": ("sbuf", [128, LW], "float8_e4m3fn_x4"),
+    "ls": ("sbuf", [128, LW], "uint8"),
     "pls": ("sbuf", [128, CW // 16], "int32"),
-    "plw": ("sbuf", [128, CW // 16], "int32"),
-    "plr": ("sbuf", [128, CW // 16], "int32"),
+    "pm0": ("sbuf", [128, CW // 16], "int32"),
+    "pm1": ("sbuf", [128, CW // 16], "int32"),
+    "pm2": ("sbuf", [128, CW // 16], "int32"),
     "offe": ("sbuf", [128, CW // 16], "uint16"),
-    "offl": ("sbuf", [128, CW // 16], "uint16"),
+    "offa": ("sbuf", [128, CW // 16], "uint16"),
     "qwb": ("sbuf", [128, QT * 512], "bfloat16"),
     "qwc": ("sbuf", [128, QT * 128], "float8_e4m3fn_x4"),
     "qws": ("sbuf", [128, QT * 128], "uint8"),
@@ -34,160 +44,129 @@ SCRATCH = {
     "rs": ("sbuf", [128, KP * QT], "float32"),
     "ysb": ("sbuf", [128, CW * QT], "float32"),
 }
-SEMAPHORES = (["xl", "sndl", "pll", "qwa", "qwb_", "own", "early", "late", "sent", "go", "store", "pa", "pb", "pc", "qf", "qn"]
-              + ["o%d" % t for t in range(4)] + ["gf%d" % t for t in range(4)] + ["gn%d" % t for t in range(4)]
-              + ["%s%d" % (a, o) for a in ("qq", "me", "ce", "ge", "ml", "cl", "gl") for o in range(QT)])
+SEMAPHORES = (["xl", "sndl", "pll", "early", "late", "sent", "go", "go1", "store", "qf", "qn", "hc", "hs",
+               "sa", "sb", "pr", "pm", "pa0", "pa1", "pa2", "pc"]
+              + ["o%d" % t for t in range(4)] + ["tf%d" % t for t in range(4)] + ["tn%d" % t for t in range(4)]
+              + ["%s%d" % (a, o) for a in ("qw", "qq", "me", "ce", "ge", "ml", "cl", "gl") for o in range(QT)])
 
 COPY = ActivationFunctionType.Copy
 
 
-def late_ranks(d, T, topo):
-    h = d // HALF * HALF
-    return [q for q in range(h, h + HALF) if topo.chip(T.cores[q]) != topo.chip(T.cores[d])]
+def half_of(r):
+    return list(range(r // HALF * HALF, r // HALF * HALF + HALF))
 
 
-def first(d, T, topo):
-    return (max(late_ranks(d, T, topo)) + 1) % N
+def order(d):
+    rest = [q for q in half_of(d) if q != d]
+    late = [q for q in range(N) if q not in half_of(d)]
+    return [d] + rest + late if d % 2 else late + rest + [d]
 
 
-def land(d, q, T, topo):
-    return CAPP * ((q - first(d, T, topo)) % N)
+def view0(d):
+    return HS - CAPP if d % 2 else LW - KP - (HS - CAPP)
+
+
+def land(d, q):
+    return view0(d) + CAPP * order(d).index(q)
+
+
+def carriers(T, topo):
+    out = {}
+    jobs = [(r, f) for r in range(N) for f in range(0, N, 2) if f not in half_of(r)]
+    for plane in (False, True):
+        for r, f in jobs:
+            c, d = T.cores[r], T.cores[f]
+            if topo.same_plane(topo.chip(c), topo.chip(d)) != plane:
+                continue
+            free = [k for k in topo.cores_of(c) if T.rank_of(k) is None and k not in out and topo.may_write(k, d)]
+            out[sorted(free, key=lambda k: topo.die(k) != topo.die(c))[0]] = (r, f)
+    return out
+
+
+def transfer(topo, dst, engs, sem, src, out):
+    rid, pid = topo.addr(dst)[:2]
+    m = 0
+    for e in engs:
+        m |= 1 << e
+    return RemoteDMATransfer(dst_ids=[DstId(rid=rid, pnc=pid)], dma_engine_mask=m, remote_sem=sem, src=src, dst=out)
+
+
+def piece(codes, planes, a, n, scale):
+    return planes[:, a:a + n] if scale else codes[:, a:a + n].bitcast(dt.uint8)
+
+
+def carrier_program(g, core, T, topo, r, f):
+    S = T.sem
+    sent = 0
+    for scale, sem in ((0, S.hc), (1, S.hs)):
+        g.wait_ge(sem, 4)
+        tr = []
+        for j in range(2):
+            e = topo.engines(core, T.cores[f + j])[scale::2]
+            e = e[len(e) // 2 * j:len(e) // 2 * (j + 1)]
+            tr.append(transfer(topo, T.cores[f + j], e, S.late, piece(T.lc, T.ls, CAPP * j, CAPP, scale),
+                               piece(T.lc, T.ls, land(f + j, r), CAPP, scale)))
+            sent += len(e)
+        g.remote_dma_fused(tr, local_sem=S.sent)
+    g.wait_ge(S.sent, sent)
 
 
 def rank_program(g, core, T, topo):
     r = T.rank_of(core)
+    car = carriers(T, topo)
     if r is None:
+        if core in car:
+            carrier_program(g, core, T, topo, *car[core])
         return
     S = T.sem
     V, A, P, Y = g.vector, g.scalar, g.tensor, g.sync
     my = r // HALF
     fh = 1 - my
-    far = list(range(HALF * fh, HALF * fh + HALF))
-    late = late_ranks(r, T, topo)
-    mate = [q for q in range(N) if q != r and topo.chip(T.cores[q]) == topo.chip(core)]
+    mate = r ^ 1
+    near = [q for q in half_of(r) if q // 2 != r // 2]
+    pairs = [near[0], r - 1] if r % 2 else [r, near[0]]
+    swapped = pairs[0] > pairs[1]
+    n0 = 0 if r % 2 else LW - HS
+    v0 = view0(r)
+    ev, lv = (0, HS) if r % 2 else (HS, 0)
     OF = [T.of0, T.of1, T.of2, T.of3]
 
-    p0 = max(0, CW // N * min(late) - DR) // 16 * 16
-    p1 = (min(CW, CW // N * max(late) + DR + CAPP + 1) + 15) // 16 * 16
-    if p1 <= CW - p0:
-        l0, l1, e0, e1 = 0, p1, p1, CW
+    if my == 0:
+        cut = (CW // N * HALF - DR) // 16 * 16
+        e0, e1, l0, l1 = 0, cut, cut, CW
     else:
-        l0, l1, e0, e1 = p0, CW, 0, p0
-    le, ll = (e1 - e0) // 16, (l1 - l0) // 16
+        cut = (CW // N * (HALF - 1) + DR + CAPP + 16) // 16 * 16
+        e0, e1, l0, l1 = cut, CW, 0, cut
+    le = (e1 - e0) // 16
 
-    for k in range(4):
-        Y.dma_start(T.sl[16 * k:16 * k + 16, :], T.snd[:, :]).then_inc(S.sndl, 16)
-        A.dma_start(T.sl[16 * k + 64:16 * k + 80, :], T.snd[:, :]).then_inc(S.sndl, 16)
+    def load_w(when):
+        for a, b, w in CFG["loads"]:
+            if w == when:
+                Y.dma_start(T.qwb[:, 512 * a:512 * b], T.qw[:, 512 * a:512 * b]).then_inc(S["qw%d" % a], 16)
+
+    Y.dma_start(T.sl[0:16, :], T.snd[:, :]).then_inc(S.sndl, 16)
+    A.dma_start(T.sl[16:32, :], T.snd[:, :]).then_inc(S.sndl, 16)
     Y.dma_start(T.xs[:, :], T.x[:, :]).then_inc(S.xl, 16)
-    Y.dma_start(T.qwb[:, 0:2048], T.qw[:, 0:2048]).then_inc(S.qwa, 16)
-    for k in range(8):
-        Y.dma_start(T.pls[16 * k:16 * k + 16, :], T.pl[:, :]).then_inc(S.pll, 16)
+    A.dma_start(T.pls[0:16, :], T.pl[:, :]).then_inc(S.pll, 16)
+    A.dma_start(T.pls[16:32, :], T.pl[:, :]).then_inc(S.pll, 16)
+    load_w("now")
+    Y.wait_ge(S.sndl, 32)
+    load_w("snd")
 
-    V.wait_ge(S.sndl, 128)
+    V.wait_ge(S.sndl, 32)
+    L = T.sl
+    if swapped:
+        L, c, w = T.sp, HS // 16 * my, PS // 16
+        V.tensor_copy(L[0:32, c:c + w], T.sl[0:32, c + w:c + 2 * w]).then_inc(S.sa, 1)
+        V.tensor_copy(L[0:32, c + w:c + 2 * w], T.sl[0:32, c:c + w]).then_inc(S.sa, 1)
+        c = HS // 16 * fh
+        V.tensor_copy(L[0:32, c:c + 2 * w], T.sl[0:32, c:c + 2 * w]).then_inc(S.sa, 1)
+        V.wait_ge(S.sa, 3)
+    for k in (32, 64, 96):
+        V.tensor_copy(L[k:k + 32, :], L[0:32, :]).then_inc(S.sb, 1)
+    V.wait_ge(S.sb, 3)
     for t in (2, 0, 3, 1):
-        V.tensor_scalar(OF[t][:, :], T.sl[:, :], 4.0, float(t), AluOpType.mult, AluOpType.add).then_inc(S["o%d" % t], 1)
-
-    def gather(tile, h, name, wait):
-        c = HS // 16 * h
-        for eng, t in ((V, 0), (A, 2), (V, 1), (A, 3)):
-            if wait:
-                eng.wait_ge(S["o%d" % t], 1)
-                if t % 2 == 0:
-                    eng.wait_ge(S.xl, 16)
-            src = T.xs[:, 0:4 * TC].indirect(OF[t][:, c:c + HS // 16])
-            if eng is V:
-                V.tensor_copy(tile[:, t:4 * HS:4], src).then_inc(S["%s%d" % (name, t)], 1)
-            else:
-                A.activation(tile[:, t:4 * HS:4], src, COPY).then_inc(S["%s%d" % (name, t)], 1)
-
-    gather(T.tf, fh, "gf", True)
-    for t in range(4):
-        V.wait_ge(S["gf%d" % t], 1)
-    V.quantize_mx(T.qfc[:, :], T.qfs[:, :], T.tf[:, :]).then_inc(S.qf, 1)
-    gather(T.tn, my, "gn", False)
-    for t in range(4):
-        V.wait_ge(S["gn%d" % t], 1)
-    V.quantize_mx(T.qnc[:, :], T.qns[:, :], T.tn[:, :]).then_inc(S.qn, 1)
-
-    def transfer(dst, engs, sem, codes, planes, scale):
-        rid, pid = topo.addr(T.cores[dst])[:2]
-        a, b = CAPP * (dst % HALF), land(dst, r, T, topo)
-        if scale:
-            s, d = planes[:, a:a + CAPP], T.ls[:, b:b + CAPP]
-        else:
-            s, d = codes[:, a:a + CAPP].bitcast(dt.uint8), T.lc[:, b:b + CAPP].bitcast(dt.uint8)
-        m = 0
-        for e in engs:
-            m |= 1 << e
-        return RemoteDMATransfer(dst_ids=[DstId(rid=rid, pnc=pid)], dma_engine_mask=m, remote_sem=sem, src=s, dst=d)
-
-    g.wait_ge(S.qf, 1)
-    sent = 0
-    for scale in (False, True):
-        tr = []
-        for i, d in enumerate(far):
-            e = topo.engines(core, T.cores[d])
-            w = len(e) // len(far)
-            tr.append(transfer(d, e[w * i:w * i + w], S.early, T.qfc, T.qfs, scale))
-            sent += w
-        g.remote_dma_fused(tr, local_sem=S.sent)
-    g.wait_ge(S.qn, 1)
-    for scale in (False, True):
-        tr, used = [], []
-        for i, d in enumerate(late):
-            e = topo.engines(core, T.cores[d])
-            w = len(e) // len(late)
-            tr.append(transfer(d, e[w * i:w * i + w], S.late, T.qnc, T.qns, scale))
-            used += e[w * i:w * i + w]
-        for d in mate:
-            e = [k for k in topo.engines(core, T.cores[d]) if k not in used]
-            tr.append(transfer(d, e, S.early, T.qnc, T.qns, scale))
-            used += e
-        sent += len(used)
-        g.remote_dma_fused(tr, local_sem=S.sent)
-    g.sem_inc(S.go, 1)
-    n_early = 2 * (8 + 8)
-    n_late = 2 * 8
-
-    a, b = CAPP * (r % HALF), land(r, r, T, topo)
-    Y.wait_ge(S.qn, 1)
-    Y.dma_start(T.lc[:, b:b + CAPP].bitcast(dt.uint8), T.qnc[:, a:a + CAPP].bitcast(dt.uint8)).then_inc(S.own, 16)
-    Y.dma_start(T.ls[:, b:b + CAPP], T.qns[:, a:a + CAPP]).then_inc(S.own, 16)
-    Y.wait_ge(S.go, 1)
-    Y.dma_start(T.qwb[:, 2048:4096], T.qw[:, 2048:4096]).then_inc(S.qwb_, 16)
-
-    def quant_w(o):
-        V.quantize_mx(T.qwc[:, 128 * o:128 * o + 128], T.qws[:, 128 * o:128 * o + 128],
-                      T.qwb[:, 512 * o:512 * o + 512]).then_inc(S["qq%d" % o], 1)
-
-    V.wait_ge(S.qwa, 16)
-    V.wait_ge(S.pll, 128)
-    rot = float(CAPP * first(r, T, topo))
-    V.tensor_scalar(T.plw[:, :], T.pls[:, :], rot, float(KP), AluOpType.is_lt, AluOpType.mult).then_inc(S.pa, 1)
-    quant_w(0)
-    quant_w(1)
-    V.wait_ge(S.pa, 1)
-    V.tensor_tensor(T.plr[:, :], T.pls[:, :], T.plw[:, :], AluOpType.add).then_inc(S.pb, 1)
-    quant_w(2)
-    quant_w(3)
-    V.wait_ge(S.pb, 1)
-    V.tensor_scalar(T.offe[:, 0:le], T.plr[:, e0 // 16:e1 // 16], rot, None, AluOpType.subtract).then_inc(S.pc, 1)
-    V.tensor_scalar(T.offl[:, 0:ll], T.plr[:, l0 // 16:l1 // 16], rot, None, AluOpType.subtract).then_inc(S.pc, 1)
-    V.wait_ge(S.qwb_, 16)
-    for o in range(4, QT):
-        quant_w(o)
-
-    P.wait_ge(S.own, 32)
-    P.wait_ge(S.early, n_early)
-    for o in range(QT):
-        P.wait_ge(S["qq%d" % o], 1)
-        P.matmul_mx(T.ps[:, 512 * o:512 * o + EARLY], T.qwc[:, 128 * o:128 * o + 128], T.qws[:, 128 * o:128 * o + 128],
-                    T.lc[:, 0:EARLY], T.ls[:, 0:EARLY], True, True).then_inc(S["me%d" % o], 1)
-    P.wait_ge(S.late, n_late)
-    for o in range(QT):
-        P.wait_ge(S["ce%d" % o], 1)
-        P.matmul_mx(T.ps[:, 512 * o:512 * o + LM], T.qwc[:, 128 * o:128 * o + 128], T.qws[:, 128 * o:128 * o + 128],
-                    T.lc[:, KP - LM:KP], T.ls[:, KP - LM:KP], True, True).then_inc(S["ml%d" % o], 1)
+        V.tensor_scalar(OF[t][:, :], L[:, :], 4.0, float(t), AluOpType.mult, AluOpType.add).then_inc(S["o%d" % t], 1)
 
     def move(eng, out, src, sem):
         if eng is V:
@@ -195,34 +174,177 @@ def rank_program(g, core, T, topo):
         else:
             A.activation(out, src, COPY).then_inc(sem, 1)
 
+    tiles = {"far": (T.tf, fh, "tf", T.qfc[:, :], T.qfs[:, :], S.qf),
+             "near": (T.tn, my, "tn", T.lc[:, n0:n0 + HS], T.ls[:, n0:n0 + HS], S.qn)}
+    rounds = ["far", "near"] if CFG["first"] == "far" else ["near", "far"]
+    V.wait_ge(S.xl, 16)
+    A.wait_ge(S.xl, 16)
+    seen = set()
+    for i, name in enumerate(rounds):
+        tile, h, sem, codes, plane, done = tiles[name]
+        c = HS // 16 * h
+        on_v = CFG["second_v"] if i else (0, 1)
+        for t in range(4):
+            eng = V if t in on_v else A
+            if (t in on_v, t) not in seen:
+                eng.wait_ge(S["o%d" % t], 1)
+                seen.add((t in on_v, t))
+            move(eng, tile[:, t:4 * HS:4], T.xs[:, 0:4 * TC].indirect(OF[t][:, c:c + HS // 16]), S["%s%d" % (sem, t)])
+        for t in range(4):
+            V.wait_ge(S["%s%d" % (sem, t)], 1)
+        V.quantize_mx(codes, plane, tile[:, :]).then_inc(done, 1)
+
+    mine = sorted((f, c) for c, (q, f) in car.items() if q == r)
+    sent = [0]
+
+    def near_col(d):
+        return n0 + PS * pairs.index(d - d % 2) + CAPP * (d % 2)
+
+    def send_far():
+        g.wait_ge(S.qf, 1)
+        for scale, sem in ((0, S.hc), (1, S.hs)):
+            tr = []
+            for j, (f, c) in enumerate(mine):
+                e = topo.engines(core, c)[scale::2]
+                e = e[len(e) // 2 * j:len(e) // 2 * (j + 1)]
+                tr.append(transfer(topo, c, e, sem, piece(T.qfc, T.qfs, CAPP * (f % HALF), PS, scale),
+                                   piece(T.lc, T.ls, 0, PS, scale)))
+                sent[0] += len(e)
+            g.remote_dma_fused(tr, local_sem=S.sent)
+
+    def send_near():
+        g.wait_ge(S.qn, 1)
+        for scale in (0, 1):
+            tr = []
+            off = topo.engines(core, T.cores[near[0]])
+            for j, d in enumerate(near + [mate]):
+                if d == mate:
+                    e = [k for k in topo.engines(core, T.cores[d]) if k not in off][1 - scale::2]
+                else:
+                    e = off[1 - scale::2]
+                    e = e[len(e) // 2 * j:len(e) // 2 * (j + 1)]
+                tr.append(transfer(topo, T.cores[d], e, S.early, piece(T.lc, T.ls, near_col(d), CAPP, scale),
+                                   piece(T.lc, T.ls, land(d, r), CAPP, scale)))
+                sent[0] += len(e)
+            g.remote_dma_fused(tr, local_sem=S.sent)
+
+    for name, sem, when in zip(rounds, (S.go1, S.go), ("go1", "go")):
+        (send_far if name == "far" else send_near)()
+        if any(w == when for a, b, w in CFG["loads"]):
+            g.sem_inc(sem, 1)
+            Y.wait_ge(sem, 1)
+            load_w(when)
+    n_early = 2 * (2 + 2 + 4)
+    n_late = 2 * 2 * HALF
+
+    def quant_w(o):
+        if any(a == o for a, b, w in CFG["loads"]):
+            V.wait_ge(S["qw%d" % o], 16)
+        V.quantize_mx(T.qwc[:, 128 * o:128 * o + 128], T.qws[:, 128 * o:128 * o + 128],
+                      T.qwb[:, 512 * o:512 * o + 512]).then_inc(S["qq%d" % o], 1)
+
+    def places(todo):
+        def fill():
+            if todo:
+                quant_w(todo.pop(0))
+        shift = [CAPP * (order(r).index(q) - q) for q in range(N)]
+        breaks = [(CAPP * q, shift[q] - shift[q - 1]) for q in range(1, N) if shift[q] != shift[q - 1]]
+        PM = [T.pm0, T.pm1, T.pm2]
+        V.wait_ge(S.pll, 32)
+        for k in (32, 64, 96):
+            V.tensor_copy(T.pls[k:k + 32, :], T.pls[0:32, :]).then_inc(S.pr, 1)
+        fill()
+        V.wait_ge(S.pr, 3)
+        for i, (b, dl) in enumerate(breaks):
+            V.tensor_scalar(PM[i][:, :], T.pls[:, :], float(b), float(dl), AluOpType.is_ge, AluOpType.mult).then_inc(S.pm, 1)
+        fill()
+        V.wait_ge(S.pm, len(breaks))
+        for i in range(len(breaks)):
+            V.tensor_tensor(T.pls[:, :], T.pls[:, :], PM[i][:, :], AluOpType.add).then_inc(S["pa%d" % i], 1)
+            fill()
+            V.wait_ge(S["pa%d" % i], 1)
+        V.tensor_scalar(T.offe[:, 0:le], T.pls[:, e0 // 16:e1 // 16], float(shift[0] - ev), None,
+                        AluOpType.add).then_inc(S.pc, 1)
+        V.tensor_scalar(T.offa[:, :], T.pls[:, :], float(shift[0]), None, AluOpType.add).then_inc(S.pc, 1)
+        while todo:
+            fill()
+
+    two = [int(k[2:]) for k in CFG["p"].split() if k[:2] == "me"]
+    staged = [int(k[2:]) for k in (CFG["v"] + " " + CFG["a"]).split() if k[:2] == "ge"]
+
+    def product(o, a, n, sem):
+        P.matmul_mx(T.ps[:, 512 * o:512 * o + n], T.qwc[:, 128 * o:128 * o + 128], T.qws[:, 128 * o:128 * o + 128],
+                    T.lc[:, v0 + a:v0 + a + n], T.ls[:, v0 + a:v0 + a + n], True, True).then_inc(sem, 1)
+
+    P.wait_ge(S.qn, 1)
+    P.wait_ge(S.early, n_early)
+    waited = False
+    for k in CFG["p"].split():
+        o = int(k[2:])
+        if k[:2] == "me":
+            P.wait_ge(S["qq%d" % o], 1)
+            product(o, ev, HS, S["me%d" % o])
+            continue
+        if not waited:
+            P.wait_ge(S.late, n_late)
+            waited = True
+        if o in two:
+            P.wait_ge(S["ce%d" % o], 1)
+            product(o, lv, HS, S["ml%d" % o])
+        else:
+            P.wait_ge(S["qq%d" % o], 1)
+            product(o, 0, KP, S["ml%d" % o])
+
     def copy_early(eng, o):
         eng.wait_ge(S["me%d" % o], 1)
-        move(eng, T.rs[:, KP * o:KP * o + EARLY], T.ps[:, 512 * o:512 * o + EARLY], S["ce%d" % o])
+        move(eng, T.rs[:, KP * o + ev:KP * o + ev + HS], T.ps[:, 512 * o:512 * o + HS], S["ce%d" % o])
 
     def gather_early(eng, o):
         eng.wait_ge(S["ce%d" % o], 1)
-        move(eng, T.ysb[:, CW * o + e0:CW * o + e1], T.rs[:, KP * o:KP * o + EARLY].indirect(T.offe[:, 0:le]), S["ge%d" % o])
+        move(eng, T.ysb[:, CW * o + e0:CW * o + e1], T.rs[:, KP * o + ev:KP * o + ev + HS].indirect(T.offe[:, 0:le]),
+             S["ge%d" % o])
 
     def copy_late(eng, o):
+        a, n = (lv, HS) if o in two else (0, KP)
         eng.wait_ge(S["ml%d" % o], 1)
-        move(eng, T.rs[:, KP * o + EARLY:KP * o + KP], T.ps[:, 512 * o + LM - 2 * CAPP:512 * o + LM], S["cl%d" % o])
+        move(eng, T.rs[:, KP * o + a:KP * o + a + n], T.ps[:, 512 * o:512 * o + n], S["cl%d" % o])
 
     def gather_late(eng, o):
+        a, b = (l0, l1) if o in staged else (0, CW)
         eng.wait_ge(S["cl%d" % o], 1)
-        move(eng, T.ysb[:, CW * o + l0:CW * o + l1], T.rs[:, KP * o:KP * o + KP].indirect(T.offl[:, 0:ll]), S["gl%d" % o])
+        move(eng, T.ysb[:, CW * o + a:CW * o + b], T.rs[:, KP * o:KP * o + KP].indirect(T.offa[:, a // 16:b // 16]),
+             S["gl%d" % o])
 
-    for eng, k in ((V, 0), (A, 1)):
-        eng.wait_ge(S.pc, 2)
-        for cp, ga in ((copy_early, gather_early), (copy_late, gather_late)):
-            cp(eng, k)
-            for o in range(k, QT - 2, 2):
-                cp(eng, o + 2)
-                ga(eng, o)
-            ga(eng, QT - 2 + k)
+    steps = {"ce": copy_early, "ge": gather_early, "cl": copy_late, "gl": gather_late}
+    for eng, seq in ((V, CFG["v"]), (A, CFG["a"])):
+        got = False
+        for k in seq.split():
+            if k[:3] == "pl:":
+                places([int(o) for o in k[3:].split(",") if o])
+            elif k[0] == "q":
+                quant_w(int(k[1:]))
+            else:
+                if k[0] == "g" and not got:
+                    eng.wait_ge(S.pc, 2)
+                    got = True
+                steps[k[:2]](eng, int(k[2:]))
 
-    for name, a, b in (("ge", e0, e1), ("gl", l0, l1)):
-        for o in range(QT):
-            Y.wait_ge(S["%s%d" % (name, o)], 1)
-            Y.dma_start(T.y[:, CW * o + a:CW * o + b], T.ysb[:, CW * o + a:CW * o + b]).then_inc(S.store, 16)
-    Y.wait_ge(S.store, 16 * 2 * QT)
-    g.wait_ge(S.sent, sent)
+    for k in CFG["y"].split():
+        o = int(k[1:])
+        if k[0] == "O":
+            a, b, sems = CW * (o + my) + e0, CW * (o + my) + e1, ["ge%d" % (o + my)]
+        elif k[0] == "P":
+            a, b, sems = CW * o + l0, CW * (o + 1) + l1, ["ge%d" % (o + fh), "gl%d" % o, "gl%d" % (o + 1)]
+        elif k[0] == "E":
+            a, b, sems = CW * o + e0, CW * o + e1, ["ge%d" % o]
+        elif k[0] == "L":
+            a, b, sems = CW * o + l0, CW * o + l1, ["gl%d" % o]
+        else:
+            bl = [o] if k[0] == "W" else [o, o + 1]
+            a, b = CW * o, CW * (bl[-1] + 1)
+            sems = ["gl%d" % j for j in bl] + ["ge%d" % j for j in bl if j in staged]
+        for s in sems:
+            Y.wait_ge(S[s], 1)
+        Y.dma_start(T.y[:, a:b], T.ysb[:, a:b]).then_inc(S.store, 16)
+    Y.wait_ge(S.store, 16 * len(CFG["y"].split()))
+    g.wait_ge(S.sent, sent[0])

@@ -5,16 +5,26 @@ N, TC, KP, CAPP, DR, CW, QT = 8, 512, 320, 40, 32, 256, 8
 HALF = N // 2
 HS = HALF * CAPP
 PS = 2 * CAPP
-LW = 448
+LW = 2 * KP - CAPP + 8
+MM = 128
+NB = 4
 
 CFG = dict(
-    first="far",
-    loads=[(0, 4, "snd"), (4, 8, "snd")],
+    order="SXN",
+    f1=128,
+    calls=[(1, "S0>a@on00 S1>b@on01 X0>c@on1"), (0, "S0>a@on0 S1>b@on1 X0>c@off"), (0, "N@off M@on"), (1, "N@off M@on"),
+           (0, "X1@off"), (1, "X1@off")],
+    carrier="off",
+    pre=40,
+    preb=(0, 1, 2, 3, 4, 5, 6, 7),
+    qfirst=3,
+    lv="c0 c2 a0 g1 c4 g3 c6 g5 a7",
+    la="c1 b0 c3 g2 c5 g4 c7 g6 b7",
+    pl8=False,
+    far_die=False,
+    loads=[(0, 4), (4, 8)],
     second_v=(0, 1),
-    v="pl:0,1,2,3,4,5,6,7 ce0 ce2 ge0 ce4 ge2 ce6 ge4 ge6 cl0 cl2 gl0 cl4 gl2 cl6 gl4 gl6",
-    a="ce1 ce3 ge1 ce5 ge3 ce7 ge5 ge7 cl1 cl3 gl1 cl5 gl3 cl7 gl5 gl7",
-    p="me0 me1 me2 me3 me4 me5 me6 me7 ml0 ml1 ml2 ml3 ml4 ml5 ml6 ml7",
-    y="O0 O2 O4 O6 P0 P2 P4 P6",
+    y="E0 E1 E2 E3 E4 E5 E6 E7 L0 L1 L2 L3 L4 L5 L6 L7",
 )
 
 SCRATCH = {
@@ -25,18 +35,13 @@ SCRATCH = {
     "of1": ("sbuf", [128, KP // 16], "uint16"),
     "of2": ("sbuf", [128, KP // 16], "uint16"),
     "of3": ("sbuf", [128, KP // 16], "uint16"),
-    "tf": ("sbuf", [128, 4 * HS], "bfloat16"),
-    "tn": ("sbuf", [128, 4 * HS], "bfloat16"),
-    "qfc": ("sbuf", [128, HS], "float8_e4m3fn_x4"),
-    "qfs": ("sbuf", [128, HS], "uint8"),
+    "tl": ("sbuf", [128, 4 * KP], "bfloat16"),
     "lc": ("sbuf", [128, LW], "float8_e4m3fn_x4"),
     "ls": ("sbuf", [128, LW], "uint8"),
     "pls": ("sbuf", [128, CW // 16], "int32"),
-    "pm0": ("sbuf", [128, CW // 16], "int32"),
-    "pm1": ("sbuf", [128, CW // 16], "int32"),
-    "pm2": ("sbuf", [128, CW // 16], "int32"),
+    "pm": ("sbuf", [128, NB * CW // 16], "int32"),
     "offe": ("sbuf", [128, CW // 16], "uint16"),
-    "offa": ("sbuf", [128, CW // 16], "uint16"),
+    "offl": ("sbuf", [128, CW // 16], "uint16"),
     "qwb": ("sbuf", [128, QT * 512], "bfloat16"),
     "qwc": ("sbuf", [128, QT * 128], "float8_e4m3fn_x4"),
     "qws": ("sbuf", [128, QT * 128], "uint8"),
@@ -44,43 +49,105 @@ SCRATCH = {
     "rs": ("sbuf", [128, KP * QT], "float32"),
     "ysb": ("sbuf", [128, CW * QT], "float32"),
 }
-SEMAPHORES = (["xl", "sndl", "pll", "early", "late", "sent", "go", "go1", "store", "qf", "qn", "hc", "hs",
-               "sa", "sb", "pr", "pm", "pa0", "pa1", "pa2", "pc"]
-              + ["o%d" % t for t in range(4)] + ["tf%d" % t for t in range(4)] + ["tn%d" % t for t in range(4)]
-              + ["%s%d" % (a, o) for a in ("qw", "qq", "me", "ce", "ge", "ml", "cl", "gl") for o in range(QT)])
+SEMAPHORES = (["xl", "sndl", "pll", "inm", "in0", "in1", "sent", "store", "q0", "q1", "h0", "h1", "sa", "sb", "pr", "pm", "pc"]
+              + ["pa%d" % t for t in range(NB)]
+              + ["%s%d" % (a, t) for a in ("o", "ta", "tb") for t in range(4)]
+              + ["%s%d" % (a, o) for a in ("qw", "qq", "mp", "cp", "m0", "c0", "g0", "m1", "c1", "g1") for o in range(QT)])
 
 COPY = ActivationFunctionType.Copy
 
 
-def half_of(r):
-    return list(range(r // HALF * HALF, r // HALF * HALF + HALF))
+def chips_of(r, T, topo):
+    me = topo.chip(T.cores[r])
+    rest = [f for f in range(0, N, 2) if f != r - r % 2]
+    plane = [f for f in rest if topo.same_plane(me, topo.chip(T.cores[f]))]
+    return sorted((f for f in rest if f not in plane), key=lambda f: f // HALF != r // HALF) + plane
 
 
-def order(d):
-    rest = [q for q in half_of(d) if q != d]
-    late = [q for q in range(N) if q not in half_of(d)]
-    return [d] + rest + late if d % 2 else late + rest + [d]
-
-
-def view0(d):
-    return HS - CAPP if d % 2 else LW - KP - (HS - CAPP)
+def stages_of(d):
+    near = [q for q in range(N) if q // HALF == d // HALF and q // 2 != d // 2]
+    far = [q for q in range(N) if q // HALF != d // HALF]
+    if d % 2:
+        return [([d, d - 1] + near, KP - CAPP), (far, KP - CAPP + HS)]
+    return [(near + [d + 1, d], LW - KP + CAPP - HS), (far, LW - KP + CAPP - KP)]
 
 
 def land(d, q):
-    return view0(d) + CAPP * order(d).index(q)
+    for k, (qs, a) in enumerate(stages_of(d)):
+        if q in qs:
+            return k, a + CAPP * qs.index(q)
+
+
+def tile_pairs(r, T, topo):
+    f = dict(zip("NXS", chips_of(r, T, topo)))
+    p = [f[k] for k in CFG["order"]] + [r - r % 2]
+    return p if r % 2 else p[::-1]
+
+
+def dests(r, name, T, topo):
+    if name == "M":
+        return [r ^ 1]
+    p = tile_pairs(r, T, topo)
+    seq = [q + j for q in p for j in (0, 1)]
+    far_end = seq if r % 2 else seq[::-1]
+    out = []
+    for i, k in enumerate(name):
+        if k in "NXS":
+            a = 2 * CFG["order"].index(k)
+            nxt = name[i + 1:i + 2]
+            out += [far_end[a + int(nxt)]] if nxt.isdigit() else far_end[a:a + 2]
+    return sorted(out, key=seq.index)
+
+
+def parse(spec):
+    out = []
+    for w in spec.split():
+        a, e = w.split("@")
+        out.append(tuple(a.split(">")) + (e,) if ">" in a else (a, None, e))
+    return out
 
 
 def carriers(T, topo):
+    jobs = []
+    for r in range(N):
+        need = {}
+        for scale, spec in CFG["calls"]:
+            for grp, h, e in parse(spec):
+                if h:
+                    need.setdefault(h, set()).update(dests(r, grp, T, topo))
+        for h, ds in need.items():
+            c = T.cores[r]
+            ok = [k for k in topo.cores_of(c) if T.rank_of(k) is None and all(topo.may_write(k, T.cores[d]) for d in ds)]
+            jobs.append((len(ok), r, h, sorted(ok, key=lambda k: (topo.die(k) == topo.die(c)) == CFG["far_die"])))
     out = {}
-    jobs = [(r, f) for r in range(N) for f in range(0, N, 2) if f not in half_of(r)]
-    for plane in (False, True):
-        for r, f in jobs:
-            c, d = T.cores[r], T.cores[f]
-            if topo.same_plane(topo.chip(c), topo.chip(d)) != plane:
-                continue
-            free = [k for k in topo.cores_of(c) if T.rank_of(k) is None and k not in out and topo.may_write(k, d)]
-            out[sorted(free, key=lambda k: topo.die(k) != topo.die(c))[0]] = (r, f)
+    for n, r, h, ok in sorted(jobs, key=lambda j: (j[0], j[2], j[1])):
+        out[[k for k in ok if k not in out][0]] = (r, h)
     return out
+
+
+def arrivals(d, T, topo):
+    sets = engine_sets(T, topo)
+    n = {"inm": 0, "in0": 0, "in1": 0}
+    for r in range(N):
+        for scale, spec in CFG["calls"]:
+            for grp, h, e in parse(spec):
+                ds = dests(r, grp, T, topo)
+                if d in ds:
+                    n["inm" if grp == "M" else "in%d" % land(d, r)[0]] += len(sets[CFG["carrier"] if h else e]) // len(ds)
+    return n
+
+
+def engine_sets(T, topo):
+    off = topo.engines(T.cores[0], T.cores[N - 1])
+    every = topo.engines(T.cores[0], T.cores[1])
+    on = [e for e in every if e not in off]
+    sets = {"off": off, "on": on, "all": every}
+    for k in list(sets):
+        e = sets[k]
+        sets.update({k + "e": e[0::2], k + "o": e[1::2], k + "0": e[:len(e) // 2], k + "1": e[len(e) // 2:]})
+    for k in ("off0", "off1", "on0", "on1"):
+        sets.update({k + "0": sets[k][:2], k + "1": sets[k][2:]})
+    return sets
 
 
 def transfer(topo, dst, engs, sem, src, out):
@@ -91,23 +158,26 @@ def transfer(topo, dst, engs, sem, src, out):
     return RemoteDMATransfer(dst_ids=[DstId(rid=rid, pnc=pid)], dma_engine_mask=m, remote_sem=sem, src=src, dst=out)
 
 
-def piece(codes, planes, a, n, scale):
-    return planes[:, a:a + n] if scale else codes[:, a:a + n].bitcast(dt.uint8)
+def piece(T, a, scale, n=CAPP):
+    return T.ls[:, a:a + n] if scale else T.lc[:, a:a + n].bitcast(dt.uint8)
 
 
-def carrier_program(g, core, T, topo, r, f):
+def carrier_program(g, core, T, topo, r, name):
     S = T.sem
+    sets = engine_sets(T, topo)
     sent = 0
-    for scale, sem in ((0, S.hc), (1, S.hs)):
-        g.wait_ge(sem, 4)
-        tr = []
-        for j in range(2):
-            e = topo.engines(core, T.cores[f + j])[scale::2]
-            e = e[len(e) // 2 * j:len(e) // 2 * (j + 1)]
-            tr.append(transfer(topo, T.cores[f + j], e, S.late, piece(T.lc, T.ls, CAPP * j, CAPP, scale),
-                               piece(T.lc, T.ls, land(f + j, r), CAPP, scale)))
-            sent += len(e)
-        g.remote_dma_fused(tr, local_sem=S.sent)
+    for scale, spec in CFG["calls"]:
+        for grp, h, e in parse(spec):
+            if h != name:
+                continue
+            ds = dests(r, grp, T, topo)
+            es = sets[CFG["carrier"]]
+            n = len(es) // len(ds)
+            g.wait_ge(S["h%d" % scale], len(sets[e]))
+            g.remote_dma_fused([transfer(topo, T.cores[d], es[n * j:n * j + n], S["in%d" % land(d, r)[0]],
+                                         piece(T, CAPP * j, scale), piece(T, land(d, r)[1], scale))
+                                for j, d in enumerate(ds)], local_sem=S.sent)
+            sent += n * len(ds)
     g.wait_ge(S.sent, sent)
 
 
@@ -122,13 +192,11 @@ def rank_program(g, core, T, topo):
     V, A, P, Y = g.vector, g.scalar, g.tensor, g.sync
     my = r // HALF
     fh = 1 - my
-    mate = r ^ 1
-    near = [q for q in half_of(r) if q // 2 != r // 2]
-    pairs = [near[0], r - 1] if r % 2 else [r, near[0]]
-    swapped = pairs[0] > pairs[1]
-    n0 = 0 if r % 2 else LW - HS
-    v0 = view0(r)
-    ev, lv = (0, HS) if r % 2 else (HS, 0)
+    pairs = tile_pairs(r, T, topo)
+    t0 = 0 if r % 2 else LW - KP
+    f1 = CFG["f1"]
+    parts = [(0, f1), (f1, KP)] if r % 2 else [(KP - f1, KP), (0, KP - f1)]
+    stages = stages_of(r)
     OF = [T.of0, T.of1, T.of2, T.of3]
 
     if my == 0:
@@ -137,36 +205,33 @@ def rank_program(g, core, T, topo):
     else:
         cut = (CW // N * (HALF - 1) + DR + CAPP + 16) // 16 * 16
         e0, e1, l0, l1 = cut, CW, 0, cut
-    le = (e1 - e0) // 16
-
-    def load_w(when):
-        for a, b, w in CFG["loads"]:
-            if w == when:
-                Y.dma_start(T.qwb[:, 512 * a:512 * b], T.qw[:, 512 * a:512 * b]).then_inc(S["qw%d" % a], 16)
 
     Y.dma_start(T.sl[0:16, :], T.snd[:, :]).then_inc(S.sndl, 16)
     A.dma_start(T.sl[16:32, :], T.snd[:, :]).then_inc(S.sndl, 16)
     Y.dma_start(T.xs[:, :], T.x[:, :]).then_inc(S.xl, 16)
-    A.dma_start(T.pls[0:16, :], T.pl[:, :]).then_inc(S.pll, 16)
-    A.dma_start(T.pls[16:32, :], T.pl[:, :]).then_inc(S.pll, 16)
-    load_w("now")
+    npl = 8 if CFG["pl8"] else 2
+    for k in range(npl):
+        A.dma_start(T.pls[16 * k:16 * k + 16, :], T.pl[:, :]).then_inc(S.pll, 16)
     Y.wait_ge(S.sndl, 32)
-    load_w("snd")
+    for a, b in CFG["loads"]:
+        Y.dma_start(T.qwb[:, 512 * a:512 * b], T.qw[:, 512 * a:512 * b]).then_inc(S["qw%d" % a], 16)
 
     V.wait_ge(S.sndl, 32)
-    L = T.sl
-    if swapped:
-        L, c, w = T.sp, HS // 16 * my, PS // 16
-        V.tensor_copy(L[0:32, c:c + w], T.sl[0:32, c + w:c + 2 * w]).then_inc(S.sa, 1)
-        V.tensor_copy(L[0:32, c + w:c + 2 * w], T.sl[0:32, c:c + w]).then_inc(S.sa, 1)
-        c = HS // 16 * fh
-        V.tensor_copy(L[0:32, c:c + 2 * w], T.sl[0:32, c:c + 2 * w]).then_inc(S.sa, 1)
-        V.wait_ge(S.sa, 3)
+    w = PS // 16
+    moves = []
+    for i, f in enumerate(pairs):
+        if moves and moves[-1][1] + moves[-1][2] == w * f // 2:
+            moves[-1][2] += w
+        else:
+            moves.append([w * i, w * f // 2, w])
+    for a, b, n in moves:
+        V.tensor_copy(T.sp[0:32, a:a + n], T.sl[0:32, b:b + n]).then_inc(S.sa, 1)
+    V.wait_ge(S.sa, len(moves))
     for k in (32, 64, 96):
-        V.tensor_copy(L[k:k + 32, :], L[0:32, :]).then_inc(S.sb, 1)
+        V.tensor_copy(T.sp[k:k + 32, :], T.sp[0:32, :]).then_inc(S.sb, 1)
     V.wait_ge(S.sb, 3)
     for t in (2, 0, 3, 1):
-        V.tensor_scalar(OF[t][:, :], L[:, :], 4.0, float(t), AluOpType.mult, AluOpType.add).then_inc(S["o%d" % t], 1)
+        V.tensor_scalar(OF[t][:, :], T.sp[:, :], 4.0, float(t), AluOpType.mult, AluOpType.add).then_inc(S["o%d" % t], 1)
 
     def move(eng, out, src, sem):
         if eng is V:
@@ -174,177 +239,161 @@ def rank_program(g, core, T, topo):
         else:
             A.activation(out, src, COPY).then_inc(sem, 1)
 
-    tiles = {"far": (T.tf, fh, "tf", T.qfc[:, :], T.qfs[:, :], S.qf),
-             "near": (T.tn, my, "tn", T.lc[:, n0:n0 + HS], T.ls[:, n0:n0 + HS], S.qn)}
-    rounds = ["far", "near"] if CFG["first"] == "far" else ["near", "far"]
     V.wait_ge(S.xl, 16)
     A.wait_ge(S.xl, 16)
     seen = set()
-    for i, name in enumerate(rounds):
-        tile, h, sem, codes, plane, done = tiles[name]
-        c = HS // 16 * h
+    for i, (a, b) in enumerate(parts):
+        sem = ("ta", "tb")[i]
         on_v = CFG["second_v"] if i else (0, 1)
         for t in range(4):
             eng = V if t in on_v else A
             if (t in on_v, t) not in seen:
                 eng.wait_ge(S["o%d" % t], 1)
                 seen.add((t in on_v, t))
-            move(eng, tile[:, t:4 * HS:4], T.xs[:, 0:4 * TC].indirect(OF[t][:, c:c + HS // 16]), S["%s%d" % (sem, t)])
+            move(eng, T.tl[:, 4 * a + t:4 * b:4], T.xs[:, 0:4 * TC].indirect(OF[t][:, a // 16:b // 16]), S["%s%d" % (sem, t)])
         for t in range(4):
             V.wait_ge(S["%s%d" % (sem, t)], 1)
-        V.quantize_mx(codes, plane, tile[:, :]).then_inc(done, 1)
+        V.quantize_mx(T.lc[:, t0 + a:t0 + b], T.ls[:, t0 + a:t0 + b], T.tl[:, 4 * a:4 * b]).then_inc(S["q%d" % i], 1)
 
-    mine = sorted((f, c) for c, (q, f) in car.items() if q == r)
-    sent = [0]
+    by = {h: c for c, (q, h) in car.items() if q == r}
+    sets = engine_sets(T, topo)
+    sent, ready = 0, 0
+    for scale, spec in CFG["calls"]:
+        tr, need = [], 1
+        for grp, h, name in parse(spec):
+            ds = dests(r, grp, T, topo)
+            cols = [PS * pairs.index(d - d % 2) + CAPP * (d % 2) for d in ds]
+            if cols[0] < parts[0][0] or cols[-1] + CAPP > parts[0][1]:
+                need = 2
+            if h:
+                n = CAPP * len(ds)
+                tr.append(transfer(topo, by[h], sets[name], S["h%d" % scale], piece(T, t0 + cols[0], scale, n),
+                                   piece(T, 0, scale, n)))
+                sent += len(sets[name])
+                continue
+            n = len(sets[name]) // len(ds)
+            for j, d in enumerate(ds):
+                k, b = land(d, r)
+                tr.append(transfer(topo, T.cores[d], sets[name][n * j:n * j + n], S.inm if grp == "M" else S["in%d" % k],
+                                   piece(T, t0 + cols[j], scale), piece(T, b, scale)))
+                sent += n
+        while ready < need:
+            g.wait_ge(S["q%d" % ready], 1)
+            ready += 1
+        g.remote_dma_fused(tr, local_sem=S.sent)
+    got = arrivals(r, T, topo)
+    n_mate, arrive = got["inm"], [got["in0"], got["in1"]]
 
-    def near_col(d):
-        return n0 + PS * pairs.index(d - d % 2) + CAPP * (d % 2)
+    todo = list(range(QT))
 
-    def send_far():
-        g.wait_ge(S.qf, 1)
-        for scale, sem in ((0, S.hc), (1, S.hs)):
-            tr = []
-            for j, (f, c) in enumerate(mine):
-                e = topo.engines(core, c)[scale::2]
-                e = e[len(e) // 2 * j:len(e) // 2 * (j + 1)]
-                tr.append(transfer(topo, c, e, sem, piece(T.qfc, T.qfs, CAPP * (f % HALF), PS, scale),
-                                   piece(T.lc, T.ls, 0, PS, scale)))
-                sent[0] += len(e)
-            g.remote_dma_fused(tr, local_sem=S.sent)
+    def quant_w():
+        if todo:
+            o = todo.pop(0)
+            if any(a == o for a, b in CFG["loads"]):
+                V.wait_ge(S["qw%d" % o], 16)
+            V.quantize_mx(T.qwc[:, 128 * o:128 * o + 128], T.qws[:, 128 * o:128 * o + 128],
+                          T.qwb[:, 512 * o:512 * o + 512]).then_inc(S["qq%d" % o], 1)
 
-    def send_near():
-        g.wait_ge(S.qn, 1)
-        for scale in (0, 1):
-            tr = []
-            off = topo.engines(core, T.cores[near[0]])
-            for j, d in enumerate(near + [mate]):
-                if d == mate:
-                    e = [k for k in topo.engines(core, T.cores[d]) if k not in off][1 - scale::2]
-                else:
-                    e = off[1 - scale::2]
-                    e = e[len(e) // 2 * j:len(e) // 2 * (j + 1)]
-                tr.append(transfer(topo, T.cores[d], e, S.early, piece(T.lc, T.ls, near_col(d), CAPP, scale),
-                                   piece(T.lc, T.ls, land(d, r), CAPP, scale)))
-                sent[0] += len(e)
-            g.remote_dma_fused(tr, local_sem=S.sent)
-
-    for name, sem, when in zip(rounds, (S.go1, S.go), ("go1", "go")):
-        (send_far if name == "far" else send_near)()
-        if any(w == when for a, b, w in CFG["loads"]):
-            g.sem_inc(sem, 1)
-            Y.wait_ge(sem, 1)
-            load_w(when)
-    n_early = 2 * (2 + 2 + 4)
-    n_late = 2 * 2 * HALF
-
-    def quant_w(o):
-        if any(a == o for a, b, w in CFG["loads"]):
-            V.wait_ge(S["qw%d" % o], 16)
-        V.quantize_mx(T.qwc[:, 128 * o:128 * o + 128], T.qws[:, 128 * o:128 * o + 128],
-                      T.qwb[:, 512 * o:512 * o + 512]).then_inc(S["qq%d" % o], 1)
-
-    def places(todo):
-        def fill():
-            if todo:
-                quant_w(todo.pop(0))
-        shift = [CAPP * (order(r).index(q) - q) for q in range(N)]
-        breaks = [(CAPP * q, shift[q] - shift[q - 1]) for q in range(1, N) if shift[q] != shift[q - 1]]
-        PM = [T.pm0, T.pm1, T.pm2]
-        V.wait_ge(S.pll, 32)
+    seq = [q for qs, a in stages for q in qs]
+    shift = [CAPP * (seq.index(q) - q) for q in range(N)]
+    breaks = [(CAPP * q, shift[q] - shift[q - 1]) for q in range(1, N) if shift[q] != shift[q - 1]]
+    U = CW // 16
+    for i in range(CFG["qfirst"]):
+        quant_w()
+    V.wait_ge(S.pll, 16 * npl)
+    if npl == 2:
         for k in (32, 64, 96):
             V.tensor_copy(T.pls[k:k + 32, :], T.pls[0:32, :]).then_inc(S.pr, 1)
-        fill()
+        quant_w()
         V.wait_ge(S.pr, 3)
-        for i, (b, dl) in enumerate(breaks):
-            V.tensor_scalar(PM[i][:, :], T.pls[:, :], float(b), float(dl), AluOpType.is_ge, AluOpType.mult).then_inc(S.pm, 1)
-        fill()
-        V.wait_ge(S.pm, len(breaks))
-        for i in range(len(breaks)):
-            V.tensor_tensor(T.pls[:, :], T.pls[:, :], PM[i][:, :], AluOpType.add).then_inc(S["pa%d" % i], 1)
-            fill()
-            V.wait_ge(S["pa%d" % i], 1)
-        V.tensor_scalar(T.offe[:, 0:le], T.pls[:, e0 // 16:e1 // 16], float(shift[0] - ev), None,
+    for i, (b, dl) in enumerate(breaks):
+        V.tensor_scalar(T.pm[:, U * i:U * i + U], T.pls[:, :], float(b), float(dl), AluOpType.is_ge,
+                        AluOpType.mult).then_inc(S.pm, 1)
+    quant_w()
+    V.wait_ge(S.pm, len(breaks))
+    for i in range(len(breaks)):
+        V.tensor_tensor(T.pls[:, :], T.pls[:, :], T.pm[:, U * i:U * i + U], AluOpType.add).then_inc(S["pa%d" % i], 1)
+        quant_w()
+        V.wait_ge(S["pa%d" % i], 1)
+    for tab, a, b in ((T.offe, e0, e1), (T.offl, l0, l1)):
+        V.tensor_scalar(tab[:, 0:(b - a) // 16], T.pls[:, a // 16:b // 16], float(shift[0]), None,
                         AluOpType.add).then_inc(S.pc, 1)
-        V.tensor_scalar(T.offa[:, :], T.pls[:, :], float(shift[0]), None, AluOpType.add).then_inc(S.pc, 1)
-        while todo:
-            fill()
+    while todo:
+        quant_w()
 
-    two = [int(k[2:]) for k in CFG["p"].split() if k[:2] == "me"]
-    staged = [int(k[2:]) for k in (CFG["v"] + " " + CFG["a"]).split() if k[:2] == "ge"]
+    pre = CFG["pre"]
+    a0, a1 = stages[0][1], stages[1][1]
 
-    def product(o, a, n, sem):
+    def views(o):
+        p = pre if o in CFG["preb"] else 0
+        n = max(MM, HS - p)
+        if r % 2:
+            return {"p": (a0 + p - MM, MM, MM - p, p, 0), "0": (a0 + HS - n, n, n - HS + p, HS - p, p), "1": (a1, HS, 0, HS, HS)}
+        return {"p": (a0 + HS - p, MM, 0, p, HS - p), "0": (a0, n, 0, HS - p, 0), "1": (a1, HS, 0, HS, HS)}
+
+    def product(k, o):
+        a, n = views(o)[k][:2]
         P.matmul_mx(T.ps[:, 512 * o:512 * o + n], T.qwc[:, 128 * o:128 * o + 128], T.qws[:, 128 * o:128 * o + 128],
-                    T.lc[:, v0 + a:v0 + a + n], T.ls[:, v0 + a:v0 + a + n], True, True).then_inc(sem, 1)
+                    T.lc[:, a:a + n], T.ls[:, a:a + n], True, True).then_inc(S["m%s%d" % (k, o)], 1)
 
-    P.wait_ge(S.qn, 1)
-    P.wait_ge(S.early, n_early)
-    waited = False
-    for k in CFG["p"].split():
-        o = int(k[2:])
-        if k[:2] == "me":
-            P.wait_ge(S["qq%d" % o], 1)
-            product(o, ev, HS, S["me%d" % o])
-            continue
-        if not waited:
-            P.wait_ge(S.late, n_late)
-            waited = True
-        if o in two:
-            P.wait_ge(S["ce%d" % o], 1)
-            product(o, lv, HS, S["ml%d" % o])
-        else:
-            P.wait_ge(S["qq%d" % o], 1)
-            product(o, 0, KP, S["ml%d" % o])
+    P.wait_ge(S.q1, 1)
+    if pre > CAPP:
+        P.wait_ge(S.inm, n_mate)
+    for o in CFG["preb"]:
+        P.wait_ge(S["qq%d" % o], 1)
+        product("p", o)
+    if pre <= CAPP:
+        P.wait_ge(S.inm, n_mate)
+    for k in range(2):
+        P.wait_ge(S["in%d" % k], arrive[k])
+        for o in range(QT):
+            P.wait_ge(S["c0%d" % o if k else ("cp%d" if o in CFG["preb"] else "qq%d") % o], 1)
+            product(str(k), o)
 
-    def copy_early(eng, o):
-        eng.wait_ge(S["me%d" % o], 1)
-        move(eng, T.rs[:, KP * o + ev:KP * o + ev + HS], T.ps[:, 512 * o:512 * o + HS], S["ce%d" % o])
+    def copy(eng, k, o):
+        a, n, u0, u, c = views(o)[k]
+        eng.wait_ge(S["m%s%d" % (k, o)], 1)
+        move(eng, T.rs[:, KP * o + c:KP * o + c + u], T.ps[:, 512 * o + u0:512 * o + u0 + u], S["c%s%d" % (k, o)])
 
-    def gather_early(eng, o):
-        eng.wait_ge(S["ce%d" % o], 1)
-        move(eng, T.ysb[:, CW * o + e0:CW * o + e1], T.rs[:, KP * o + ev:KP * o + ev + HS].indirect(T.offe[:, 0:le]),
-             S["ge%d" % o])
+    def gather(eng, k, o, a=None, b=None):
+        tab, p0, p1 = ((T.offe, e0, e1), (T.offl, l0, l1))[k]
+        a, b = (p0, p1) if a is None else (a, b)
+        eng.wait_ge(S["c%d%d" % (k, o)], 1)
+        move(eng, T.ysb[:, CW * o + a:CW * o + b],
+             T.rs[:, KP * o:KP * o + HS * k + HS].indirect(tab[:, (a - p0) // 16:(b - p0) // 16]), S["g%d%d" % (k, o)])
 
-    def copy_late(eng, o):
-        a, n = (lv, HS) if o in two else (0, KP)
-        eng.wait_ge(S["ml%d" % o], 1)
-        move(eng, T.rs[:, KP * o + a:KP * o + a + n], T.ps[:, 512 * o:512 * o + n], S["cl%d" % o])
-
-    def gather_late(eng, o):
-        a, b = (l0, l1) if o in staged else (0, CW)
-        eng.wait_ge(S["cl%d" % o], 1)
-        move(eng, T.ysb[:, CW * o + a:CW * o + b], T.rs[:, KP * o:KP * o + KP].indirect(T.offa[:, a // 16:b // 16]),
-             S["gl%d" % o])
-
-    steps = {"ce": copy_early, "ge": gather_early, "cl": copy_late, "gl": gather_late}
-    for eng, seq in ((V, CFG["v"]), (A, CFG["a"])):
-        got = False
-        for k in seq.split():
-            if k[:3] == "pl:":
-                places([int(o) for o in k[3:].split(",") if o])
-            elif k[0] == "q":
-                quant_w(int(k[1:]))
+    for o in CFG["preb"]:
+        copy(A, "p", o)
+    halves = [int(w[1]) for w in (CFG["lv"] + " " + CFG["la"]).split() if w[0] == "a"]
+    cut2 = l0 + 96
+    for eng, e, late in ((V, 0, CFG["lv"]), (A, 1, CFG["la"])):
+        bl = list(range(e, QT, 2))
+        for i in range(len(bl) + 1):
+            if i < len(bl):
+                copy(eng, "0", bl[i])
+            if i == 1:
+                eng.wait_ge(S.pc, 2)
+            if i:
+                gather(eng, 0, bl[i - 1])
+        for w in late.split():
+            o = int(w[1])
+            if w[0] == "c":
+                copy(eng, "1", o)
             else:
-                if k[0] == "g" and not got:
-                    eng.wait_ge(S.pc, 2)
-                    got = True
-                steps[k[:2]](eng, int(k[2:]))
+                gather(eng, 1, o, *{"g": (l0, l1), "a": (l0, cut2), "b": (cut2, l1)}[w[0]])
 
     for k in CFG["y"].split():
         o = int(k[1:])
         if k[0] == "O":
-            a, b, sems = CW * (o + my) + e0, CW * (o + my) + e1, ["ge%d" % (o + my)]
+            a, b, sems = CW * (o + my) + e0, CW * (o + my) + e1, ["g0%d" % (o + my)]
         elif k[0] == "P":
-            a, b, sems = CW * o + l0, CW * (o + 1) + l1, ["ge%d" % (o + fh), "gl%d" % o, "gl%d" % (o + 1)]
+            a, b, sems = CW * o + l0, CW * (o + 1) + l1, ["g0%d" % (o + fh), "g1%d" % o, "g1%d" % (o + 1)]
         elif k[0] == "E":
-            a, b, sems = CW * o + e0, CW * o + e1, ["ge%d" % o]
-        elif k[0] == "L":
-            a, b, sems = CW * o + l0, CW * o + l1, ["gl%d" % o]
+            a, b, sems = CW * o + e0, CW * o + e1, ["g0%d" % o]
         else:
-            bl = [o] if k[0] == "W" else [o, o + 1]
-            a, b = CW * o, CW * (bl[-1] + 1)
-            sems = ["gl%d" % j for j in bl] + ["ge%d" % j for j in bl if j in staged]
-        for s in sems:
-            Y.wait_ge(S[s], 1)
+            a, b, sems = CW * o + l0, CW * o + l1, ["g1%d" % o]
+        for x in sems:
+            Y.wait_ge(S[x], 2 if x[1] == "1" and int(x[2]) in halves else 1)
         Y.dma_start(T.y[:, a:b], T.ysb[:, a:b]).then_inc(S.store, 16)
     Y.wait_ge(S.store, 16 * len(CFG["y"].split()))
-    g.wait_ge(S.sent, sent[0])
+    g.wait_ge(S.sent, sent)

@@ -5,53 +5,57 @@ N, TC, KP, CAPP, DR, CW, QT = 8, 512, 320, 40, 32, 256, 8
 HALF = N // 2
 HS = HALF * CAPP
 PS = 2 * CAPP
-LW = 2 * KP - CAPP + 8
+NE = CW - HS
 MM = 128
 NB = 4
 
 CFG = dict(
-    order="SXN",
-    f1=128,
-    calls=[(1, "S0>a@on00 S1>b@on01 X0>c@on1"), (0, "S0>a@on0 S1>b@on1 X0>c@off"), (0, "N@off M@on"), (1, "N@off M@on"),
-           (0, "X1@off"), (1, "X1@off")],
-    carrier="off",
-    pre=40,
-    preb=(0, 1, 2, 3, 4, 5, 6, 7),
+    gv="00 01 10 q0 20 21 q1 30 q2 33 w q3",
+    ga="02 03 11 12 13 22 23 31 32",
+    calls=[(1, "X0>c@off"), (1, "S0>a@offe S1>b@offo"), (0, "N@off S0>a@on0e S1>b@on0o X0>c@on1"), (1, "N@off M@on1"),
+           (0, "X1@off M@on"), (1, "X1@off")],
+    carrier={"A": (False, True, "off", "off"), "B": (False, True, "off", "off"), "a": (False, True, "off", "off"), "b": (False, False, "off", "off"), "c": (False, False, "off", "off")},
     qfirst=3,
-    lv="c0 c2 a0 g1 c4 g3 c6 g5 a7",
-    la="c1 b0 c3 g2 c5 g4 c7 g6 b7",
-    pl8=False,
-    far_die=False,
+    eorder=(0, 1, 2, 3, 4, 5, 6, 7),
+    ev="c0 c2 g0 c4 g2 c6 g4 g6",
+    ea="c1 c3 g1 c5 g3 c7 g5 g7",
+    lv="c0 c2 b0 g1 c4 g3 c6 g5 b6 a7",
+    la="c1 a0 c3 g2 c5 g4 c7 a6 b7",
     loads=[(0, 4), (4, 8)],
-    second_v=(0, 1),
     y="E0 E1 E2 E3 E4 E5 E6 E7 L0 L1 L2 L3 L4 L5 L6 L7",
 )
+NP = 4
+FW = 2 * MM
+AREA = [0, MM, 2 * MM, 3 * MM, 4 * MM]
+L0 = AREA[-1]
+LW = L0 + KP - CAPP
 
 SCRATCH = {
     "xs": ("sbuf", [128, 4 * TC], "bfloat16"),
     "sl": ("sbuf", [128, KP // 16], "int32"),
-    "sp": ("sbuf", [128, KP // 16], "int32"),
     "of0": ("sbuf", [128, KP // 16], "uint16"),
     "of1": ("sbuf", [128, KP // 16], "uint16"),
     "of2": ("sbuf", [128, KP // 16], "uint16"),
     "of3": ("sbuf", [128, KP // 16], "uint16"),
-    "tl": ("sbuf", [128, 4 * KP], "bfloat16"),
+    "tl": ("sbuf", [128, 4 * (FW + MM)], "bfloat16"),
     "lc": ("sbuf", [128, LW], "float8_e4m3fn_x4"),
     "ls": ("sbuf", [128, LW], "uint8"),
     "pls": ("sbuf", [128, CW // 16], "int32"),
     "pm": ("sbuf", [128, NB * CW // 16], "int32"),
     "offe": ("sbuf", [128, CW // 16], "uint16"),
-    "offl": ("sbuf", [128, CW // 16], "uint16"),
+    "offl": ("sbuf", [128, HS // 8], "uint16"),
     "qwb": ("sbuf", [128, QT * 512], "bfloat16"),
     "qwc": ("sbuf", [128, QT * 128], "float8_e4m3fn_x4"),
     "qws": ("sbuf", [128, QT * 128], "uint8"),
     "ps": ("psum", [128, 512 * QT], "float32"),
     "rs": ("sbuf", [128, KP * QT], "float32"),
+    "jk": ("sbuf", [128, 2048], "int32"),
+    "jf": ("sbuf", [128, 4096], "float32"),
     "ysb": ("sbuf", [128, CW * QT], "float32"),
 }
-SEMAPHORES = (["xl", "sndl", "pll", "inm", "in0", "in1", "sent", "store", "q0", "q1", "h0", "h1", "sa", "sb", "pr", "pm", "pc"]
-              + ["pa%d" % t for t in range(NB)]
-              + ["%s%d" % (a, t) for a in ("o", "ta", "tb") for t in range(4)]
+SEMAPHORES = (["jj", "z", "xl", "sndl", "pll", "inm", "in0", "in1", "sent", "store", "h0", "h1", "sb", "pr", "pm", "pc"]
+              + ["pa%d" % t for t in range(NB)] + ["q%d" % k for k in range(NP)] + ["o%d" % t for t in range(4)]
+              + ["t%d%d" % (k, t) for k in range(NP) for t in range(4)]
               + ["%s%d" % (a, o) for a in ("qw", "qq", "mp", "cp", "m0", "c0", "g0", "m1", "c1", "g1") for o in range(QT)])
 
 COPY = ActivationFunctionType.Copy
@@ -65,38 +69,40 @@ def chips_of(r, T, topo):
 
 
 def stages_of(d):
-    near = [q for q in range(N) if q // HALF == d // HALF and q // 2 != d // 2]
-    far = [q for q in range(N) if q // HALF != d // HALF]
-    if d % 2:
-        return [([d, d - 1] + near, KP - CAPP), (far, KP - CAPP + HS)]
-    return [(near + [d + 1, d], LW - KP + CAPP - HS), (far, LW - KP + CAPP - KP)]
+    h = d - d % HALF
+    return [[h + (d + k) % HALF for k in range(1, HALF)], [q for q in range(N) if q // HALF != d // HALF]]
 
 
 def land(d, q):
-    for k, (qs, a) in enumerate(stages_of(d)):
-        if q in qs:
-            return k, a + CAPP * qs.index(q)
-
-
-def tile_pairs(r, T, topo):
-    f = dict(zip("NXS", chips_of(r, T, topo)))
-    p = [f[k] for k in CFG["order"]] + [r - r % 2]
-    return p if r % 2 else p[::-1]
+    near, far = stages_of(d)
+    return int(q in far), L0 + CAPP * (near + far).index(q)
 
 
 def dests(r, name, T, topo):
-    if name == "M":
-        return [r ^ 1]
-    p = tile_pairs(r, T, topo)
-    seq = [q + j for q in p for j in (0, 1)]
-    far_end = seq if r % 2 else seq[::-1]
-    out = []
-    for i, k in enumerate(name):
-        if k in "NXS":
-            a = 2 * CFG["order"].index(k)
-            nxt = name[i + 1:i + 2]
-            out += [far_end[a + int(nxt)]] if nxt.isdigit() else far_end[a:a + 2]
-    return sorted(out, key=seq.index)
+    n, x, s = chips_of(r, T, topo)
+    flip = r % 2
+    return {"M": [r ^ 1], "N": [n, n + 1], "S": [s, s + 1], "X": [x, x + 1], "N0": [n + flip], "N1": [n + 1 - flip],
+            "Sa": [s], "Sb": [s + 1], "S0": [s + flip], "S1": [s + 1 - flip], "X0": [x + (x > s)], "X1": [x + (x < s)]}[name]
+
+
+def layout(r, T, topo):
+    f = HS * (1 - r // HALF)
+    low = dests(r, "X0", T, topo)[0] % HALF > 0
+    x0, s = [(f + a, f + b, a) if low else (f + HS - b, f + HS - a, FW - b) for a, b in ((96, HS), (0, 96))]
+    n, o = [(CAPP * p // 32 * 32, CAPP * p + PS) for p in (dests(r, "N", T, topo)[0], r - r % 2)]
+    runs = [x0, s, n + (FW,), o + (HS if low else FW - HS - o[1] + o[0],)]
+    far = [(a, b) if low else (FW - b, FW - a) for a, b in ((96, 96 + MM), (0, MM), (MM, FW), (HS, FW))]
+    parts = [far[0] + ([0],), far[1] + ([0, 1],), (FW, FW + MM, [2]), far[2] + ([0, 3],)]
+    return runs, parts, [far[3], (FW + PS, FW + MM)]
+
+
+def source(r, ds, T, topo):
+    runs, parts, _ = layout(r, T, topo)
+    for k, (q0, q1, need) in enumerate(parts):
+        col = {s: c + s - a for a, b, c in (runs[j] for j in reversed(need)) for s in range(a, b)}
+        cols = [col.get(s, -1) for s in range(CAPP * ds[0], CAPP * (ds[0] + len(ds)))]
+        if q0 <= min(cols) and max(cols) < q1 and cols == list(range(cols[0], cols[0] + len(cols))):
+            return k, AREA[k] + cols[0] - q0
 
 
 def parse(spec):
@@ -116,9 +122,14 @@ def carriers(T, topo):
                 if h:
                     need.setdefault(h, set()).update(dests(r, grp, T, topo))
         for h, ds in need.items():
-            c = T.cores[r]
-            ok = [k for k in topo.cores_of(c) if T.rank_of(k) is None and all(topo.may_write(k, T.cores[d]) for d in ds)]
-            jobs.append((len(ok), r, h, sorted(ok, key=lambda k: (topo.die(k) == topo.die(c)) == CFG["far_die"])))
+            if h.isupper() and r % 2:
+                continue
+            there, same = CFG["carrier"][h][:2]
+            c = T.cores[min(ds) if there else r]
+            ok = [k for k in topo.cores_of(c) if T.rank_of(k) is None and topo.may_write(T.cores[r], k)
+                  and all(topo.may_write(k, T.cores[d]) for d in ds)]
+            ok = [k for k in ok if (topo.die(k) == topo.die(c)) == same] + [k for k in ok if (topo.die(k) == topo.die(c)) != same]
+            jobs.append((len(ok) - same, r, h, ok))
     out = {}
     for n, r, h, ok in sorted(jobs, key=lambda j: (j[0], j[2], j[1])):
         out[[k for k in ok if k not in out][0]] = (r, h)
@@ -132,8 +143,8 @@ def arrivals(d, T, topo):
         for scale, spec in CFG["calls"]:
             for grp, h, e in parse(spec):
                 ds = dests(r, grp, T, topo)
-                if d in ds:
-                    n["inm" if grp == "M" else "in%d" % land(d, r)[0]] += len(sets[CFG["carrier"] if h else e]) // len(ds)
+                if d in ds and not (h and h.isupper() and r % 2):
+                    n["inm" if grp == "M" else "in%d" % land(d, r)[0]] += len(sets[CFG["carrier"][h][2 + scale] if h else e]) // len(ds)
     return n
 
 
@@ -146,7 +157,7 @@ def engine_sets(T, topo):
         e = sets[k]
         sets.update({k + "e": e[0::2], k + "o": e[1::2], k + "0": e[:len(e) // 2], k + "1": e[len(e) // 2:]})
     for k in ("off0", "off1", "on0", "on1"):
-        sets.update({k + "0": sets[k][:2], k + "1": sets[k][2:]})
+        sets.update({k + "0": sets[k][:2], k + "1": sets[k][2:], k + "e": sets[k][0::2], k + "o": sets[k][1::2]})
     return sets
 
 
@@ -171,11 +182,12 @@ def carrier_program(g, core, T, topo, r, name):
             if h != name:
                 continue
             ds = dests(r, grp, T, topo)
-            es = sets[CFG["carrier"]]
+            es = sets[CFG["carrier"][h][2 + scale]]
             n = len(es) // len(ds)
-            g.wait_ge(S["h%d" % scale], len(sets[e]))
+            k = 2 if h.isupper() else 1
+            g.wait_ge(S["h%d" % scale], k * len(sets[e]))
             g.remote_dma_fused([transfer(topo, T.cores[d], es[n * j:n * j + n], S["in%d" % land(d, r)[0]],
-                                         piece(T, CAPP * j, scale), piece(T, land(d, r)[1], scale))
+                                         piece(T, k * CAPP * j, scale, k * CAPP), piece(T, land(d, r)[1], scale, k * CAPP))
                                 for j, d in enumerate(ds)], local_sem=S.sent)
             sent += n * len(ds)
     g.wait_ge(S.sent, sent)
@@ -190,99 +202,39 @@ def rank_program(g, core, T, topo):
         return
     S = T.sem
     V, A, P, Y = g.vector, g.scalar, g.tensor, g.sync
-    my = r // HALF
-    fh = 1 - my
-    pairs = tile_pairs(r, T, topo)
-    t0 = 0 if r % 2 else LW - KP
-    f1 = CFG["f1"]
-    parts = [(0, f1), (f1, KP)] if r % 2 else [(KP - f1, KP), (0, KP - f1)]
-    stages = stages_of(r)
+    near, far = stages_of(r)
     OF = [T.of0, T.of1, T.of2, T.of3]
 
-    if my == 0:
-        cut = (CW // N * HALF - DR) // 16 * 16
-        e0, e1, l0, l1 = 0, cut, cut, CW
+    if r < HALF:
+        e0, e1, l0, l1 = 0, CW - HS, CW - HS, CW
     else:
-        cut = (CW // N * (HALF - 1) + DR + CAPP + 16) // 16 * 16
-        e0, e1, l0, l1 = cut, CW, 0, cut
+        e0, e1, l0, l1 = HS, CW, 0, HS
 
+    Y.dma_start(T.xs[0:32, :], T.x[0:32, :]).then_inc(S.xl, 16)
     Y.dma_start(T.sl[0:16, :], T.snd[:, :]).then_inc(S.sndl, 16)
     A.dma_start(T.sl[16:32, :], T.snd[:, :]).then_inc(S.sndl, 16)
-    Y.dma_start(T.xs[:, :], T.x[:, :]).then_inc(S.xl, 16)
-    npl = 8 if CFG["pl8"] else 2
-    for k in range(npl):
-        A.dma_start(T.pls[16 * k:16 * k + 16, :], T.pl[:, :]).then_inc(S.pll, 16)
-    Y.wait_ge(S.sndl, 32)
+    Y.dma_start(T.xs[32:128, :], T.x[32:128, :]).then_inc(S.xl, 16)
+    for k in range(2):
+        Y.dma_start(T.pls[16 * k:16 * k + 16, :], T.pl[:, :]).then_inc(S.pll, 16)
     for a, b in CFG["loads"]:
         Y.dma_start(T.qwb[:, 512 * a:512 * b], T.qw[:, 512 * a:512 * b]).then_inc(S["qw%d" % a], 16)
 
+    runs, parts, zero = layout(r, T, topo)
+    for a, b in zero:
+        V.memset(T.tl[:, 4 * a:4 * b], 0.0).then_inc(S.z, 1)
+    V.wait_ge(S.z, len(zero))
     V.wait_ge(S.sndl, 32)
-    w = PS // 16
-    moves = []
-    for i, f in enumerate(pairs):
-        if moves and moves[-1][1] + moves[-1][2] == w * f // 2:
-            moves[-1][2] += w
-        else:
-            moves.append([w * i, w * f // 2, w])
-    for a, b, n in moves:
-        V.tensor_copy(T.sp[0:32, a:a + n], T.sl[0:32, b:b + n]).then_inc(S.sa, 1)
-    V.wait_ge(S.sa, len(moves))
     for k in (32, 64, 96):
-        V.tensor_copy(T.sp[k:k + 32, :], T.sp[0:32, :]).then_inc(S.sb, 1)
+        V.tensor_copy(T.sl[k:k + 32, :], T.sl[0:32, :]).then_inc(S.sb, 1)
     V.wait_ge(S.sb, 3)
     for t in (2, 0, 3, 1):
-        V.tensor_scalar(OF[t][:, :], T.sp[:, :], 4.0, float(t), AluOpType.mult, AluOpType.add).then_inc(S["o%d" % t], 1)
+        V.tensor_scalar(OF[t][:, :], T.sl[:, :], 4.0, float(t), AluOpType.mult, AluOpType.add).then_inc(S["o%d" % t], 1)
 
     def move(eng, out, src, sem):
         if eng is V:
             V.tensor_copy(out, src).then_inc(sem, 1)
         else:
             A.activation(out, src, COPY).then_inc(sem, 1)
-
-    V.wait_ge(S.xl, 16)
-    A.wait_ge(S.xl, 16)
-    seen = set()
-    for i, (a, b) in enumerate(parts):
-        sem = ("ta", "tb")[i]
-        on_v = CFG["second_v"] if i else (0, 1)
-        for t in range(4):
-            eng = V if t in on_v else A
-            if (t in on_v, t) not in seen:
-                eng.wait_ge(S["o%d" % t], 1)
-                seen.add((t in on_v, t))
-            move(eng, T.tl[:, 4 * a + t:4 * b:4], T.xs[:, 0:4 * TC].indirect(OF[t][:, a // 16:b // 16]), S["%s%d" % (sem, t)])
-        for t in range(4):
-            V.wait_ge(S["%s%d" % (sem, t)], 1)
-        V.quantize_mx(T.lc[:, t0 + a:t0 + b], T.ls[:, t0 + a:t0 + b], T.tl[:, 4 * a:4 * b]).then_inc(S["q%d" % i], 1)
-
-    by = {h: c for c, (q, h) in car.items() if q == r}
-    sets = engine_sets(T, topo)
-    sent, ready = 0, 0
-    for scale, spec in CFG["calls"]:
-        tr, need = [], 1
-        for grp, h, name in parse(spec):
-            ds = dests(r, grp, T, topo)
-            cols = [PS * pairs.index(d - d % 2) + CAPP * (d % 2) for d in ds]
-            if cols[0] < parts[0][0] or cols[-1] + CAPP > parts[0][1]:
-                need = 2
-            if h:
-                n = CAPP * len(ds)
-                tr.append(transfer(topo, by[h], sets[name], S["h%d" % scale], piece(T, t0 + cols[0], scale, n),
-                                   piece(T, 0, scale, n)))
-                sent += len(sets[name])
-                continue
-            n = len(sets[name]) // len(ds)
-            for j, d in enumerate(ds):
-                k, b = land(d, r)
-                tr.append(transfer(topo, T.cores[d], sets[name][n * j:n * j + n], S.inm if grp == "M" else S["in%d" % k],
-                                   piece(T, t0 + cols[j], scale), piece(T, b, scale)))
-                sent += n
-        while ready < need:
-            g.wait_ge(S["q%d" % ready], 1)
-            ready += 1
-        g.remote_dma_fused(tr, local_sem=S.sent)
-    got = arrivals(r, T, topo)
-    n_mate, arrive = got["inm"], [got["in0"], got["in1"]]
 
     todo = list(range(QT))
 
@@ -294,106 +246,157 @@ def rank_program(g, core, T, topo):
             V.quantize_mx(T.qwc[:, 128 * o:128 * o + 128], T.qws[:, 128 * o:128 * o + 128],
                           T.qwb[:, 512 * o:512 * o + 512]).then_inc(S["qq%d" % o], 1)
 
-    seq = [q for qs, a in stages for q in qs]
+    for eng, words in ((V, CFG["gv"]), (A, CFG["ga"])):
+        eng.wait_ge(S.xl, 32)
+        seen = set()
+
+        def once(x):
+            if x not in seen:
+                seen.add(x)
+                eng.wait_ge(S[x], 1)
+
+        for w in words.split():
+            if w == "w":
+                quant_w()
+            elif w[0] == "q":
+                k = int(w[1])
+                c, d, need = parts[k]
+                for j in need:
+                    for t in range(4):
+                        once("t%d%d" % (j, t))
+                V.quantize_mx(T.lc[:, AREA[k]:AREA[k + 1]], T.ls[:, AREA[k]:AREA[k + 1]], T.tl[:, 4 * c:4 * d]).then_inc(S[w], 1)
+            else:
+                (a, b, c), t = runs[int(w[0])], int(w[1])
+                once("o%d" % t)
+                if int(w[0]) > 2:
+                    once("q0")
+                move(eng, T.tl[:, 4 * c + t:4 * (c + b - a):4], T.xs[:, 0:4 * TC].indirect(OF[t][:, a // 16:b // 16]), S["t" + w])
+
+    by = {h: c for c, (q, h) in car.items() if q == (r - r % 2 if h.isupper() else r)}
+    sets = engine_sets(T, topo)
+    sent, ready = 0, 0
+    for scale, spec in CFG["calls"]:
+        tr, need = [], 0
+        for grp, h, name in parse(spec):
+            ds = dests(r, grp, T, topo)
+            if h:
+                k, a = source(r, ds, T, topo)
+                need = max(need, k + 1)
+                n = CAPP * len(ds)
+                tr.append(transfer(topo, by[h], sets[name], S["h%d" % scale], piece(T, a, scale, n),
+                                   piece(T, CAPP * (r % 2) * h.isupper(), scale, n)))
+                sent += len(sets[name])
+                continue
+            n = len(sets[name]) // len(ds)
+            for j, d in enumerate(ds):
+                k, a = source(r, [d], T, topo)
+                need = max(need, k + 1)
+                st, b = land(d, r)
+                tr.append(transfer(topo, T.cores[d], sets[name][n * j:n * j + n], S.inm if grp == "M" else S["in%d" % st],
+                                   piece(T, a, scale), piece(T, b, scale)))
+                sent += n
+        while ready < need:
+            g.wait_ge(S["q%d" % ready], 1)
+            ready += 1
+        g.remote_dma_fused(tr, local_sem=S.sent)
+    got = arrivals(r, T, topo)
+
+    seq = [r] + near + far
     shift = [CAPP * (seq.index(q) - q) for q in range(N)]
     breaks = [(CAPP * q, shift[q] - shift[q - 1]) for q in range(1, N) if shift[q] != shift[q - 1]]
     U = CW // 16
     for i in range(CFG["qfirst"]):
         quant_w()
-    V.wait_ge(S.pll, 16 * npl)
-    if npl == 2:
-        for k in (32, 64, 96):
-            V.tensor_copy(T.pls[k:k + 32, :], T.pls[0:32, :]).then_inc(S.pr, 1)
-        quant_w()
-        V.wait_ge(S.pr, 3)
+    V.wait_ge(S.pll, 32)
+    for k in (32, 64, 96):
+        V.tensor_copy(T.pls[k:k + 32, :], T.pls[0:32, :]).then_inc(S.pr, 1)
+    quant_w()
+    V.wait_ge(S.pr, 3)
     for i, (b, dl) in enumerate(breaks):
         V.tensor_scalar(T.pm[:, U * i:U * i + U], T.pls[:, :], float(b), float(dl), AluOpType.is_ge,
                         AluOpType.mult).then_inc(S.pm, 1)
     quant_w()
-    V.wait_ge(S.pm, len(breaks))
+    if breaks:
+        V.wait_ge(S.pm, len(breaks))
     for i in range(len(breaks)):
         V.tensor_tensor(T.pls[:, :], T.pls[:, :], T.pm[:, U * i:U * i + U], AluOpType.add).then_inc(S["pa%d" % i], 1)
         quant_w()
         V.wait_ge(S["pa%d" % i], 1)
-    for tab, a, b in ((T.offe, e0, e1), (T.offl, l0, l1)):
-        V.tensor_scalar(tab[:, 0:(b - a) // 16], T.pls[:, a // 16:b // 16], float(shift[0]), None,
+    for tab, a, b, c in ((T.offe[:, 0:NE // 16], e0, e1, 0), (T.offl[:, 0:HS // 16], l0, l1, 0)):
+        V.tensor_scalar(tab, T.pls[:, a // 16:b // 16], float(shift[0] + c), None,
                         AluOpType.add).then_inc(S.pc, 1)
     while todo:
         quant_w()
 
-    pre = CFG["pre"]
-    a0, a1 = stages[0][1], stages[1][1]
+    ko, ao = source(r, [r], T, topo)
+    vo = min(ao, AREA[ko + 1] - MM)
+    ne = HS - CAPP
+    view = {"p": (vo, MM, ao - vo, CAPP, 0), "0": (L0 + ne - MM, MM, MM - ne, ne, CAPP), "1": (L0 + ne, HS, 0, HS, HS)}
 
-    def views(o):
-        p = pre if o in CFG["preb"] else 0
-        n = max(MM, HS - p)
-        if r % 2:
-            return {"p": (a0 + p - MM, MM, MM - p, p, 0), "0": (a0 + HS - n, n, n - HS + p, HS - p, p), "1": (a1, HS, 0, HS, HS)}
-        return {"p": (a0 + HS - p, MM, 0, p, HS - p), "0": (a0, n, 0, HS - p, 0), "1": (a1, HS, 0, HS, HS)}
+    def base(o):
+        return KP * o
 
     def product(k, o):
-        a, n = views(o)[k][:2]
+        a, n = view[k][:2]
         P.matmul_mx(T.ps[:, 512 * o:512 * o + n], T.qwc[:, 128 * o:128 * o + 128], T.qws[:, 128 * o:128 * o + 128],
                     T.lc[:, a:a + n], T.ls[:, a:a + n], True, True).then_inc(S["m%s%d" % (k, o)], 1)
 
-    P.wait_ge(S.q1, 1)
-    if pre > CAPP:
-        P.wait_ge(S.inm, n_mate)
-    for o in CFG["preb"]:
+    P.wait_ge(S["q%d" % ko], 1)
+    for o in range(QT):
         P.wait_ge(S["qq%d" % o], 1)
         product("p", o)
-    if pre <= CAPP:
-        P.wait_ge(S.inm, n_mate)
+    P.wait_ge(S["q%d" % (NP - 1)], 1)
+    P.wait_ge(S.inm, got["inm"])
     for k in range(2):
-        P.wait_ge(S["in%d" % k], arrive[k])
-        for o in range(QT):
-            P.wait_ge(S["c0%d" % o if k else ("cp%d" if o in CFG["preb"] else "qq%d") % o], 1)
+        P.wait_ge(S["in%d" % k], got["in%d" % k])
+        for o in range(QT) if k else CFG["eorder"]:
+            P.wait_ge(S[("c0%d" if k else "cp%d") % o], 1)
             product(str(k), o)
 
     def copy(eng, k, o):
-        a, n, u0, u, c = views(o)[k]
+        a, n, u0, u, c = view[k]
         eng.wait_ge(S["m%s%d" % (k, o)], 1)
-        move(eng, T.rs[:, KP * o + c:KP * o + c + u], T.ps[:, 512 * o + u0:512 * o + u0 + u], S["c%s%d" % (k, o)])
+        move(eng, T.rs[:, base(o) + c:base(o) + c + u], T.ps[:, 512 * o + u0:512 * o + u0 + u], S["c%s%d" % (k, o)])
 
-    def gather(eng, k, o, a=None, b=None):
-        tab, p0, p1 = ((T.offe, e0, e1), (T.offl, l0, l1))[k]
-        a, b = (p0, p1) if a is None else (a, b)
-        eng.wait_ge(S["c%d%d" % (k, o)], 1)
-        move(eng, T.ysb[:, CW * o + a:CW * o + b],
-             T.rs[:, KP * o:KP * o + HS * k + HS].indirect(tab[:, (a - p0) // 16:(b - p0) // 16]), S["g%d%d" % (k, o)])
+    def early(eng, o, n):
+        for j in range(o, o + n):
+            eng.wait_ge(S["c0%d" % j], 1)
+        move(eng, T.ysb[:, CW * o + e0:CW * o + e1], T.rs[:, base(o):base(o) + HS * n].indirect(T.offe[:, 0:n * NE // 16]), S["g0%d" % o])
 
-    for o in CFG["preb"]:
+    def late(eng, o, a, b):
+        eng.wait_ge(S["c1%d" % o], 1)
+        move(eng, T.ysb[:, CW * o + l0 + a:CW * o + l0 + b], T.rs[:, base(o):base(o) + KP].indirect(T.offl[:, a // 16:b // 16]), S["g1%d" % o])
+
+    for o in range(QT):
         copy(A, "p", o)
     halves = [int(w[1]) for w in (CFG["lv"] + " " + CFG["la"]).split() if w[0] == "a"]
-    cut2 = l0 + 96
-    for eng, e, late in ((V, 0, CFG["lv"]), (A, 1, CFG["la"])):
-        bl = list(range(e, QT, 2))
-        for i in range(len(bl) + 1):
-            if i < len(bl):
-                copy(eng, "0", bl[i])
-            if i == 1:
+    pairs = [int(w[1]) for w in (CFG["ev"] + " " + CFG["ea"]).split() if w[0] == "G"]
+    lpairs = [int(w[1]) for w in (CFG["lv"] + " " + CFG["la"]).split() if w[0] == "G"]
+    for eng, ew, lw in ((V, CFG["ev"], CFG["lv"]), (A, CFG["ea"], CFG["la"])):
+        first = True
+        for w in ew.split():
+            o = int(w[1])
+            if w[0] == "c":
+                copy(eng, "0", o)
+                continue
+            if first:
                 eng.wait_ge(S.pc, 2)
-            if i:
-                gather(eng, 0, bl[i - 1])
-        for w in late.split():
+                first = False
+            early(eng, o, 2 if w[0] == "G" else 1)
+        for w in lw.split():
             o = int(w[1])
             if w[0] == "c":
                 copy(eng, "1", o)
             else:
-                gather(eng, 1, o, *{"g": (l0, l1), "a": (l0, cut2), "b": (cut2, l1)}[w[0]])
+                late(eng, o, *{"g": (0, HS), "G": (0, KP), "a": (0, NE), "b": (NE, HS)}[w[0]])
 
     for k in CFG["y"].split():
         o = int(k[1:])
-        if k[0] == "O":
-            a, b, sems = CW * (o + my) + e0, CW * (o + my) + e1, ["g0%d" % (o + my)]
-        elif k[0] == "P":
-            a, b, sems = CW * o + l0, CW * (o + 1) + l1, ["g0%d" % (o + fh), "g1%d" % o, "g1%d" % (o + 1)]
-        elif k[0] == "E":
-            a, b, sems = CW * o + e0, CW * o + e1, ["g0%d" % o]
-        else:
-            a, b, sems = CW * o + l0, CW * o + l1, ["g1%d" % o]
-        for x in sems:
-            Y.wait_ge(S[x], 2 if x[1] == "1" and int(x[2]) in halves else 1)
-        Y.dma_start(T.y[:, a:b], T.ysb[:, a:b]).then_inc(S.store, 16)
+        if k[0] in "EW":
+            Y.wait_ge(S["g0%d" % o], 1)
+        if k[0] in "LW":
+            Y.wait_ge(S["g1%d" % o], 2 if o in halves else 1)
+        a, b = {"E": (e0, e1), "L": (l0, l1), "W": (0, CW)}[k[0]]
+        Y.dma_start(T.y[:, CW * o + a:CW * o + b], T.ysb[:, CW * o + a:CW * o + b]).then_inc(S.store, 16)
     Y.wait_ge(S.store, 16 * len(CFG["y"].split()))
     g.wait_ge(S.sent, sent)

from concourse.bass import DstId, RemoteDMATransfer
from concourse.mybir import dt, AluOpType, ActivationFunctionType

N, TC, KP, CAPP, DR, CW, QT = 8, 512, 320, 40, 32, 256, 8
HALF = N // 2
HS = HALF * CAPP
PS = 2 * CAPP
NE = CW - HS
MM = 128
NB = 4

CFG = dict(
    gv="00 01 10 q0 20 21 q1 30 q2 33 w q3",
    ga="02 03 11 12 13 22 23 31 32",
    calls=[(1, "X0>c@off"), (1, "S0>a@offe S1>b@offo"), (0, "N@off S0>a@on0e S1>b@on0o X0>c@on1"), (1, "N@off M@on1"),
           (0, "X1@off M@on"), (1, "X1@off")],
    carrier={"A": (False, True, "off", "off"), "B": (False, True, "off", "off"), "a": (False, True, "off", "off"), "b": (False, False, "off", "off"), "c": (False, False, "off", "off")},
    qfirst=3,
    eorder=(0, 1, 2, 3, 4, 5, 6, 7),
    ev="c0 c2 g0 c4 g2 c6 g4 g6",
    ea="c1 c3 g1 c5 g3 c7 g5 g7",
    lv="c0 c2 b0 g1 c4 g3 c6 g5 b6 a7",
    la="c1 a0 c3 g2 c5 g4 c7 a6 b7",
    loads=[(0, 4), (4, 8)],
    y="E0 E1 E2 E3 E4 E5 E6 E7 L0 L1 L2 L3 L4 L5 L6 L7",
)
NP = 4
FW = 2 * MM
AREA = [0, MM, 2 * MM, 3 * MM, 4 * MM]
L0 = AREA[-1]
LW = L0 + KP - CAPP

SCRATCH = {
    "xs": ("sbuf", [128, 4 * TC], "bfloat16"),
    "sl": ("sbuf", [128, KP // 16], "int32"),
    "of0": ("sbuf", [128, KP // 16], "uint16"),
    "of1": ("sbuf", [128, KP // 16], "uint16"),
    "of2": ("sbuf", [128, KP // 16], "uint16"),
    "of3": ("sbuf", [128, KP // 16], "uint16"),
    "tl": ("sbuf", [128, 4 * (FW + MM)], "bfloat16"),
    "lc": ("sbuf", [128, LW], "float8_e4m3fn_x4"),
    "ls": ("sbuf", [128, LW], "uint8"),
    "pls": ("sbuf", [128, CW // 16], "int32"),
    "pm": ("sbuf", [128, NB * CW // 16], "int32"),
    "offe": ("sbuf", [128, CW // 16], "uint16"),
    "offl": ("sbuf", [128, HS // 8], "uint16"),
    "qwb": ("sbuf", [128, QT * 512], "bfloat16"),
    "qwc": ("sbuf", [128, QT * 128], "float8_e4m3fn_x4"),
    "qws": ("sbuf", [128, QT * 128], "uint8"),
    "ps": ("psum", [128, 512 * QT], "float32"),
    "rs": ("sbuf", [128, KP * QT], "float32"),
    "jk": ("sbuf", [128, 2048], "int32"),
    "jf": ("sbuf", [128, 4096], "float32"),
    "ysb": ("sbuf", [128, CW * QT], "float32"),
}
SEMAPHORES = (["jj", "z", "xl", "sndl", "pll", "inm", "in0", "in1", "sent", "store", "h0", "h1", "sb", "pr", "pm", "pc"]
              + ["pa%d" % t for t in range(NB)] + ["q%d" % k for k in range(NP)] + ["o%d" % t for t in range(4)]
              + ["t%d%d" % (k, t) for k in range(NP) for t in range(4)]
              + ["%s%d" % (a, o) for a in ("qw", "qq", "mp", "cp", "m0", "c0", "g0", "m1", "c1", "g1") for o in range(QT)])

COPY = ActivationFunctionType.Copy


def chips_of(r, T, topo):
    me = topo.chip(T.cores[r])
    rest = [f for f in range(0, N, 2) if f != r - r % 2]
    plane = [f for f in rest if topo.same_plane(me, topo.chip(T.cores[f]))]
    return sorted((f for f in rest if f not in plane), key=lambda f: f // HALF != r // HALF) + plane


def stages_of(d):
    h = d - d % HALF
    return [[h + (d + k) % HALF for k in range(1, HALF)], [q for q in range(N) if q // HALF != d // HALF]]


def land(d, q):
    near, far = stages_of(d)
    return int(q in far), L0 + CAPP * (near + far).index(q)


def dests(r, name, T, topo):
    n, x, s = chips_of(r, T, topo)
    flip = r % 2
    return {"M": [r ^ 1], "N": [n, n + 1], "S": [s, s + 1], "X": [x, x + 1], "N0": [n + flip], "N1": [n + 1 - flip],
            "Sa": [s], "Sb": [s + 1], "S0": [s + flip], "S1": [s + 1 - flip], "X0": [x + (x > s)], "X1": [x + (x < s)]}[name]


def layout(r, T, topo):
    f = HS * (1 - r // HALF)
    low = dests(r, "X0", T, topo)[0] % HALF > 0
    x0, s = [(f + a, f + b, a) if low else (f + HS - b, f + HS - a, FW - b) for a, b in ((96, HS), (0, 96))]
    n, o = [(CAPP * p // 32 * 32, CAPP * p + PS) for p in (dests(r, "N", T, topo)[0], r - r % 2)]
    runs = [x0, s, n + (FW,), o + (HS if low else FW - HS - o[1] + o[0],)]
    far = [(a, b) if low else (FW - b, FW - a) for a, b in ((96, 96 + MM), (0, MM), (MM, FW), (HS, FW))]
    parts = [far[0] + ([0],), far[1] + ([0, 1],), (FW, FW + MM, [2]), far[2] + ([0, 3],)]
    return runs, parts, [far[3], (FW + PS, FW + MM)]


def source(r, ds, T, topo):
    runs, parts, _ = layout(r, T, topo)
    for k, (q0, q1, need) in enumerate(parts):
        col = {s: c + s - a for a, b, c in (runs[j] for j in reversed(need)) for s in range(a, b)}
        cols = [col.get(s, -1) for s in range(CAPP * ds[0], CAPP * (ds[0] + len(ds)))]
        if q0 <= min(cols) and max(cols) < q1 and cols == list(range(cols[0], cols[0] + len(cols))):
            return k, AREA[k] + cols[0] - q0


def parse(spec):
    out = []
    for w in spec.split():
        a, e = w.split("@")
        out.append(tuple(a.split(">")) + (e,) if ">" in a else (a, None, e))
    return out


def carriers(T, topo):
    jobs = []
    for r in range(N):
        need = {}
        for scale, spec in CFG["calls"]:
            for grp, h, e in parse(spec):
                if h:
                    need.setdefault(h, set()).update(dests(r, grp, T, topo))
        for h, ds in need.items():
            if h.isupper() and r % 2:
                continue
            there, same = CFG["carrier"][h][:2]
            c = T.cores[min(ds) if there else r]
            ok = [k for k in topo.cores_of(c) if T.rank_of(k) is None and topo.may_write(T.cores[r], k)
                  and all(topo.may_write(k, T.cores[d]) for d in ds)]
            ok = [k for k in ok if (topo.die(k) == topo.die(c)) == same] + [k for k in ok if (topo.die(k) == topo.die(c)) != same]
            jobs.append((len(ok) - same, r, h, ok))
    out = {}
    for n, r, h, ok in sorted(jobs, key=lambda j: (j[0], j[2], j[1])):
        out[[k for k in ok if k not in out][0]] = (r, h)
    return out


def arrivals(d, T, topo):
    sets = engine_sets(T, topo)
    n = {"inm": 0, "in0": 0, "in1": 0}
    for r in range(N):
        for scale, spec in CFG["calls"]:
            for grp, h, e in parse(spec):
                ds = dests(r, grp, T, topo)
                if d in ds and not (h and h.isupper() and r % 2):
                    n["inm" if grp == "M" else "in%d" % land(d, r)[0]] += len(sets[CFG["carrier"][h][2 + scale] if h else e]) // len(ds)
    return n


def engine_sets(T, topo):
    off = topo.engines(T.cores[0], T.cores[N - 1])
    every = topo.engines(T.cores[0], T.cores[1])
    on = [e for e in every if e not in off]
    sets = {"off": off, "on": on, "all": every}
    for k in list(sets):
        e = sets[k]
        sets.update({k + "e": e[0::2], k + "o": e[1::2], k + "0": e[:len(e) // 2], k + "1": e[len(e) // 2:]})
    for k in ("off0", "off1", "on0", "on1"):
        sets.update({k + "0": sets[k][:2], k + "1": sets[k][2:], k + "e": sets[k][0::2], k + "o": sets[k][1::2]})
    return sets


def transfer(topo, dst, engs, sem, src, out):
    rid, pid = topo.addr(dst)[:2]
    m = 0
    for e in engs:
        m |= 1 << e
    return RemoteDMATransfer(dst_ids=[DstId(rid=rid, pnc=pid)], dma_engine_mask=m, remote_sem=sem, src=src, dst=out)


def piece(T, a, scale, n=CAPP):
    return T.ls[:, a:a + n] if scale else T.lc[:, a:a + n].bitcast(dt.uint8)


def carrier_program(g, core, T, topo, r, name):
    S = T.sem
    sets = engine_sets(T, topo)
    sent = 0
    for scale, spec in CFG["calls"]:
        for grp, h, e in parse(spec):
            if h != name:
                continue
            ds = dests(r, grp, T, topo)
            es = sets[CFG["carrier"][h][2 + scale]]
            n = len(es) // len(ds)
            k = 2 if h.isupper() else 1
            g.wait_ge(S["h%d" % scale], k * len(sets[e]))
            g.remote_dma_fused([transfer(topo, T.cores[d], es[n * j:n * j + n], S["in%d" % land(d, r)[0]],
                                         piece(T, k * CAPP * j, scale, k * CAPP), piece(T, land(d, r)[1], scale, k * CAPP))
                                for j, d in enumerate(ds)], local_sem=S.sent)
            sent += n * len(ds)
    g.wait_ge(S.sent, sent)


def rank_program(g, core, T, topo):
    r = T.rank_of(core)
    car = carriers(T, topo)
    if r is None:
        if core in car:
            carrier_program(g, core, T, topo, *car[core])
        return
    S = T.sem
    V, A, P, Y = g.vector, g.scalar, g.tensor, g.sync
    near, far = stages_of(r)
    OF = [T.of0, T.of1, T.of2, T.of3]

    if r < HALF:
        e0, e1, l0, l1 = 0, CW - HS, CW - HS, CW
    else:
        e0, e1, l0, l1 = HS, CW, 0, HS

    Y.dma_start(T.xs[0:32, :], T.x[0:32, :]).then_inc(S.xl, 16)
    Y.dma_start(T.sl[0:16, :], T.snd[:, :]).then_inc(S.sndl, 16)
    A.dma_start(T.sl[16:32, :], T.snd[:, :]).then_inc(S.sndl, 16)
    Y.dma_start(T.xs[32:128, :], T.x[32:128, :]).then_inc(S.xl, 16)
    for k in range(2):
        Y.dma_start(T.pls[16 * k:16 * k + 16, :], T.pl[:, :]).then_inc(S.pll, 16)
    for a, b in CFG["loads"]:
        Y.dma_start(T.qwb[:, 512 * a:512 * b], T.qw[:, 512 * a:512 * b]).then_inc(S["qw%d" % a], 16)

    runs, parts, zero = layout(r, T, topo)
    for a, b in zero:
        V.memset(T.tl[:, 4 * a:4 * b], 0.0).then_inc(S.z, 1)
    V.wait_ge(S.z, len(zero))
    V.wait_ge(S.sndl, 32)
    for k in (32, 64, 96):
        V.tensor_copy(T.sl[k:k + 32, :], T.sl[0:32, :]).then_inc(S.sb, 1)
    V.wait_ge(S.sb, 3)
    for t in (2, 0, 3, 1):
        V.tensor_scalar(OF[t][:, :], T.sl[:, :], 4.0, float(t), AluOpType.mult, AluOpType.add).then_inc(S["o%d" % t], 1)

    def move(eng, out, src, sem):
        if eng is V:
            V.tensor_copy(out, src).then_inc(sem, 1)
        else:
            A.activation(out, src, COPY).then_inc(sem, 1)

    todo = list(range(QT))

    def quant_w():
        if todo:
            o = todo.pop(0)
            if any(a == o for a, b in CFG["loads"]):
                V.wait_ge(S["qw%d" % o], 16)
            V.quantize_mx(T.qwc[:, 128 * o:128 * o + 128], T.qws[:, 128 * o:128 * o + 128],
                          T.qwb[:, 512 * o:512 * o + 512]).then_inc(S["qq%d" % o], 1)

    for eng, words in ((V, CFG["gv"]), (A, CFG["ga"])):
        eng.wait_ge(S.xl, 32)
        seen = set()

        def once(x):
            if x not in seen:
                seen.add(x)
                eng.wait_ge(S[x], 1)

        for w in words.split():
            if w == "w":
                quant_w()
            elif w[0] == "q":
                k = int(w[1])
                c, d, need = parts[k]
                for j in need:
                    for t in range(4):
                        once("t%d%d" % (j, t))
                V.quantize_mx(T.lc[:, AREA[k]:AREA[k + 1]], T.ls[:, AREA[k]:AREA[k + 1]], T.tl[:, 4 * c:4 * d]).then_inc(S[w], 1)
            else:
                (a, b, c), t = runs[int(w[0])], int(w[1])
                once("o%d" % t)
                if int(w[0]) > 2:
                    once("q0")
                move(eng, T.tl[:, 4 * c + t:4 * (c + b - a):4], T.xs[:, 0:4 * TC].indirect(OF[t][:, a // 16:b // 16]), S["t" + w])

    by = {h: c for c, (q, h) in car.items() if q == (r - r % 2 if h.isupper() else r)}
    sets = engine_sets(T, topo)
    sent, ready = 0, 0
    for scale, spec in CFG["calls"]:
        tr, need = [], 0
        for grp, h, name in parse(spec):
            ds = dests(r, grp, T, topo)
            if h:
                k, a = source(r, ds, T, topo)
                need = max(need, k + 1)
                n = CAPP * len(ds)
                tr.append(transfer(topo, by[h], sets[name], S["h%d" % scale], piece(T, a, scale, n),
                                   piece(T, CAPP * (r % 2) * h.isupper(), scale, n)))
                sent += len(sets[name])
                continue
            n = len(sets[name]) // len(ds)
            for j, d in enumerate(ds):
                k, a = source(r, [d], T, topo)
                need = max(need, k + 1)
                st, b = land(d, r)
                tr.append(transfer(topo, T.cores[d], sets[name][n * j:n * j + n], S.inm if grp == "M" else S["in%d" % st],
                                   piece(T, a, scale), piece(T, b, scale)))
                sent += n
        while ready < need:
            g.wait_ge(S["q%d" % ready], 1)
            ready += 1
        g.remote_dma_fused(tr, local_sem=S.sent)
    got = arrivals(r, T, topo)

    seq = [r] + near + far
    shift = [CAPP * (seq.index(q) - q) for q in range(N)]
    breaks = [(CAPP * q, shift[q] - shift[q - 1]) for q in range(1, N) if shift[q] != shift[q - 1]]
    U = CW // 16
    for i in range(CFG["qfirst"]):
        quant_w()
    V.wait_ge(S.pll, 32)
    for k in (32, 64, 96):
        V.tensor_copy(T.pls[k:k + 32, :], T.pls[0:32, :]).then_inc(S.pr, 1)
    quant_w()
    V.wait_ge(S.pr, 3)
    for i, (b, dl) in enumerate(breaks):
        V.tensor_scalar(T.pm[:, U * i:U * i + U], T.pls[:, :], float(b), float(dl), AluOpType.is_ge,
                        AluOpType.mult).then_inc(S.pm, 1)
    quant_w()
    if breaks:
        V.wait_ge(S.pm, len(breaks))
    for i in range(len(breaks)):
        V.tensor_tensor(T.pls[:, :], T.pls[:, :], T.pm[:, U * i:U * i + U], AluOpType.add).then_inc(S["pa%d" % i], 1)
        quant_w()
        V.wait_ge(S["pa%d" % i], 1)
    for tab, a, b, c in ((T.offe[:, 0:NE // 16], e0, e1, 0), (T.offl[:, 0:HS // 16], l0, l1, 0)):
        V.tensor_scalar(tab, T.pls[:, a // 16:b // 16], float(shift[0] + c), None,
                        AluOpType.add).then_inc(S.pc, 1)
    while todo:
        quant_w()

    ko, ao = source(r, [r], T, topo)
    vo = min(ao, AREA[ko + 1] - MM)
    ne = HS - CAPP
    view = {"p": (vo, MM, ao - vo, CAPP, 0), "0": (L0 + ne - MM, MM, MM - ne, ne, CAPP), "1": (L0 + ne, HS, 0, HS, HS)}

    def base(o):
        return KP * o

    def product(k, o):
        a, n = view[k][:2]
        P.matmul_mx(T.ps[:, 512 * o:512 * o + n], T.qwc[:, 128 * o:128 * o + 128], T.qws[:, 128 * o:128 * o + 128],
                    T.lc[:, a:a + n], T.ls[:, a:a + n], True, True).then_inc(S["m%s%d" % (k, o)], 1)

    P.wait_ge(S["q%d" % ko], 1)
    for o in range(QT):
        P.wait_ge(S["qq%d" % o], 1)
        product("p", o)
    P.wait_ge(S["q%d" % (NP - 1)], 1)
    P.wait_ge(S.inm, got["inm"])
    for k in range(2):
        P.wait_ge(S["in%d" % k], got["in%d" % k])
        for o in range(QT) if k else CFG["eorder"]:
            P.wait_ge(S[("c0%d" if k else "cp%d") % o], 1)
            product(str(k), o)

    def copy(eng, k, o):
        a, n, u0, u, c = view[k]
        eng.wait_ge(S["m%s%d" % (k, o)], 1)
        move(eng, T.rs[:, base(o) + c:base(o) + c + u], T.ps[:, 512 * o + u0:512 * o + u0 + u], S["c%s%d" % (k, o)])

    def early(eng, o, n):
        for j in range(o, o + n):
            eng.wait_ge(S["c0%d" % j], 1)
        move(eng, T.ysb[:, CW * o + e0:CW * o + e1], T.rs[:, base(o):base(o) + HS * n].indirect(T.offe[:, 0:n * NE // 16]), S["g0%d" % o])

    def late(eng, o, a, b):
        eng.wait_ge(S["c1%d" % o], 1)
        move(eng, T.ysb[:, CW * o + l0 + a:CW * o + l0 + b], T.rs[:, base(o):base(o) + KP].indirect(T.offl[:, a // 16:b // 16]), S["g1%d" % o])

    for o in range(QT):
        copy(A, "p", o)
    halves = [int(w[1]) for w in (CFG["lv"] + " " + CFG["la"]).split() if w[0] == "a"]
    pairs = [int(w[1]) for w in (CFG["ev"] + " " + CFG["ea"]).split() if w[0] == "G"]
    lpairs = [int(w[1]) for w in (CFG["lv"] + " " + CFG["la"]).split() if w[0] == "G"]
    for eng, ew, lw in ((V, CFG["ev"], CFG["lv"]), (A, CFG["ea"], CFG["la"])):
        first = True
        for w in ew.split():
            o = int(w[1])
            if w[0] == "c":
                copy(eng, "0", o)
                continue
            if first:
                eng.wait_ge(S.pc, 2)
                first = False
            early(eng, o, 2 if w[0] == "G" else 1)
        for w in lw.split():
            o = int(w[1])
            if w[0] == "c":
                copy(eng, "1", o)
            else:
                late(eng, o, *{"g": (0, HS), "G": (0, KP), "a": (0, NE), "b": (NE, HS)}[w[0]])

    for k in CFG["y"].split():
        o = int(k[1:])
        if k[0] in "EW":
            Y.wait_ge(S["g0%d" % o], 1)
        if k[0] in "LW":
            Y.wait_ge(S["g1%d" % o], 2 if o in halves else 1)
        a, b = {"E": (e0, e1), "L": (l0, l1), "W": (0, CW)}[k[0]]
        Y.dma_start(T.y[:, CW * o + a:CW * o + b], T.ysb[:, CW * o + a:CW * o + b]).then_inc(S.store, 16)
    Y.wait_ge(S.store, 16 * len(CFG["y"].split()))
    g.wait_ge(S.sent, sent)
